import numpy as np
import ml_dtypes


def mxq(x, axis, fmt="e4m3"):
    dtype, down = {"e4m3": (ml_dtypes.float8_e4m3fn, 7), "e5m2": (ml_dtypes.float8_e5m2, 14)}[fmt]
    v = np.moveaxis(np.asarray(x, np.float32).astype(ml_dtypes.bfloat16).astype(np.float64), axis, -1)
    blocks = v.reshape(v.shape[:-1] + (-1, 32))
    amax = np.abs(blocks).max(-1, keepdims=True)
    byte = np.maximum(np.where(amax > 0, np.frexp(amax)[1] - 1 + 127, 0) - down, 1)
    scale = np.exp2(byte - 127.0)
    codes = (blocks / scale).astype(np.float32).astype(dtype).astype(np.float64)
    return np.moveaxis((codes * scale).reshape(v.shape), -1, axis)


WIDE = False


def mx_kscale(k):
    if not WIDE:
        return np.ones(k)
    levels = np.array([10, -10, 5, -5, 0])
    if k % 512:
        return np.exp2(np.random.permutation(np.resize(levels, k // 32))).repeat(32)
    a = np.empty((k // 512, 16))
    for p in range(k // 512):
        a[p, :8] = np.random.permutation(np.resize(levels, 8))
        for g in range(8):
            far = levels[np.abs(levels - a[p, g]) >= 10]
            a[p, g + 8] = far[np.random.randint(len(far))]
    return np.exp2(a.ravel()).repeat(32)


def f64(x):
    return np.asarray(x).astype(np.float64)


def striped(idx):
    return np.tile(idx.reshape(-1, 16).T, (8, 1)).astype(np.uint16)


def unstriped(offs):
    return offs[:16].T.reshape(-1).astype(np.int64)


E2M1 = np.array([0.0, 0.5, 1.0, 1.5, 2.0, 3.0, 4.0, 6.0, -0.0, -0.5, -1.0, -1.5, -2.0, -3.0, -4.0, -6.0])


def pack_weight(w, fmt):
    k, n = w.shape
    w = f64(np.asarray(w, np.float32).astype(ml_dtypes.bfloat16)).reshape(k // 32, 32, n)
    amax = np.abs(w).max(1)
    if fmt == "e4m3":
        byte = np.frexp(amax)[1] - 1 + 127 - 7
    else:
        mant, ex = np.frexp(amax / 6.0)
        byte = np.where(mant > 0.5, ex, ex - 1) + 127
    byte = np.clip(np.where(amax > 0, byte, 1), 1, 254)
    scaled = (w * np.exp2(127.0 - byte)[:, None, :]).reshape(k, n).astype(np.float32)
    by_word = np.ascontiguousarray(scaled.reshape(k // 512, 128, 4, n).transpose(0, 1, 3, 2))
    if fmt == "e4m3":
        words = by_word.astype(ml_dtypes.float8_e4m3fn).view(np.uint8)
    else:
        c = by_word.astype(ml_dtypes.float4_e2m1fn).view(np.uint8) & 0xF
        words = (c[..., 0::2] | (c[..., 1::2] << 4)).reshape(k // 512, 128, 2 * n)
    return np.ascontiguousarray(words), np.ascontiguousarray(byte.astype(np.uint8).reshape(k // 512, 16, n))


def unpack_weight(words, scales, fmt):
    g, _, n = scales.shape
    words = np.ascontiguousarray(words).reshape(g, 128, n, -1)
    if fmt == "e4m3":
        vals = words.view(ml_dtypes.float8_e4m3fn).astype(np.float64)
    else:
        nib = np.empty((g, 128, n, 4), np.uint8)
        nib[..., 0::2] = words & 0xF
        nib[..., 1::2] = words >> 4
        vals = E2M1[nib]
    vals = vals * np.repeat(np.exp2(scales.astype(np.float64) - 127.0), 8, axis=1)[..., None]
    return vals.transpose(0, 1, 3, 2).reshape(g * 512, n)


def gelu(v):
    return 0.5 * v * (1.0 + np.tanh(np.sqrt(2.0 / np.pi) * (v + 0.044715 * v**3)))


K, H, N, T, S, T2 = 1536, 1024, 512, 2048, 1024, 2048

def setup_inputs():
    n = np.random.standard_normal
    s = mx_kscale(K)[:, None]
    u = mx_kscale(H)[:, None]
    tab_words, tab_scales = pack_weight(n((K, T)) * s, "e4m3")
    w1 = (n((K, H)) / np.sqrt(K) / s * u.T).astype(np.float32)
    w2_words, w2_scales = pack_weight(1.5 * n((H, N)) / np.sqrt(H) / u, "e2m1")
    s0 = (0.4 * n(H) * u[:, 0]).astype(np.float32)
    lo = (-0.6 * np.exp(0.2 * n(H)) * u[:, 0]).astype(np.float32)
    hi = (0.8 * np.exp(0.2 * n(H)) * u[:, 0]).astype(np.float32)
    f0 = (0.5 * n(N)).astype(np.float32)
    wgo = np.exp(0.3 * n((128, S))).astype(np.float32)
    offs = striped(np.random.permutation(T)[:S])
    offs2 = striped(np.random.permutation(T2)[:S])
    return {"tab_words": tab_words, "tab_scales": tab_scales, "w1": w1, "w2_words": w2_words, "w2_scales": w2_scales,
            "s0": s0, "lo": lo, "hi": hi, "f0": f0, "wgo": wgo, "offs": offs, "offs2": offs2}

def reference(tab_words, tab_scales, w1, w2_words, w2_scales, s0, lo, hi, f0, wgo, offs, offs2):
    v = unpack_weight(tab_words, tab_scales, "e4m3")[:, unstriped(offs)]
    w2 = unpack_weight(w2_words, w2_scales, "e2m1")
    trial = (mxq(f64(w1), 0, "e4m3").T @ v) + f64(s0)[:, None]
    h = np.minimum(np.maximum(trial, f64(lo)[:, None]), f64(hi)[:, None])
    y = (w2.T @ mxq(h, 0, "e4m3")) + f64(f0)[:, None]
    out = np.zeros((N, T2))
    out[:, unstriped(offs2)] = np.tile(f64(wgo), (N // 128, 1)) * y
    return out

@@ -1,0 +1,202 @@
+from contextlib import ExitStack
+
+import concourse.mybir as mybir
+
+K, H, N, T, S, T2 = 1536, 1024, 512, 2048, 1024, 2048
+FLOPS = 2 * K * H * S + 2 * H * N * S
+
+F32 = mybir.dt.float32
+BF16 = mybir.dt.bfloat16
+I32 = mybir.dt.int32
+U32 = mybir.dt.uint32
+U16 = mybir.dt.uint16
+U8 = mybir.dt.uint8
+FP8X4 = mybir.dt.float8_e4m3fn_x4
+FP4X4 = mybir.dt.float4_e2m1fn_x4
+ALU = mybir.AluOpType
+IDENT = mybir.ActivationFunctionType.Identity
+
+P = 128
+PACK = 4
+PASS = P * PACK
+KP = K // PASS
+HP = H // PASS
+NT = N // P
+
+
+def tile_list_yield_clipped_forces_kernel(tc, tab_words, tab_scales, w1, w2_words, w2_scales,
+                                                   s0, lo, hi, f0, wgo, offs, offs2, out):
+    nc = tc.nc
+    with ExitStack() as ctx:
+        keep = ctx.enter_context(tc.tile_pool(name="keep", bufs=1))
+        ring = ctx.enter_context(tc.tile_pool(name="ring", bufs=2))
+        psum = ctx.enter_context(tc.psum_pool(name="psum", bufs=1))
+
+        gather_list = keep.tile([P, S // 16], U16, name="gather_list")
+        scatter_list = keep.tile([P, S // 16], U16, name="scatter_list")
+        table = [keep.tile([P, T], I32, name="table%d" % a) for a in range(KP)]
+        table_sc = keep.tile([P, T // 4], I32, name="table_sc")
+        v_codes = [keep.tile([P, S], U32, name="v_codes%d" % a, align_bytes=64) for a in range(KP)]
+        v_sc = keep.tile([P, S], U8, name="v_sc", align_bytes=64)
+        w1_raw = {}
+        w1_codes = {}
+        w1_sc = {}
+        for b in range(HP):
+            for a in range(KP):
+                w1_raw[b, a] = keep.tile([P, PACK, PASS], F32, name="w1_raw%d%d" % (b, a))
+                w1_codes[b, a] = keep.tile([P, PASS], U32, name="w1_codes%d%d" % (b, a), align_bytes=64)
+                w1_sc[b, a] = keep.tile([P, PASS], U8, name="w1_sc%d%d" % (b, a), align_bytes=64)
+        w2_codes = keep.tile([P, HP, N // 2], I32, name="w2_codes", align_bytes=64)
+        w2_sc = keep.tile([P, HP, N // 4], I32, name="w2_sc", align_bytes=64)
+        s0_sb = keep.tile([P, HP, PACK], F32, name="s0_sb")
+        lo_sb = keep.tile([P, HP, PACK], F32, name="lo_sb")
+        hi_sb = keep.tile([P, HP, PACK], F32, name="hi_sb")
+        f0_sb = keep.tile([P, NT], F32, name="f0_sb")
+        wgo_sb = keep.tile([P, S], F32, name="wgo_sb")
+        h_codes = [keep.tile([P, S], U32, name="h_codes%d" % b, align_bytes=64) for b in range(HP)]
+        h_sc = [keep.tile([P, S], U8, name="h_sc%d" % b, align_bytes=64) for b in range(HP)]
+        y_sb = [keep.tile([P, S], F32, name="y_sb%d" % nt) for nt in range(NT)]
+        window = [keep.tile([P, T2], F32, name="window%d" % nt) for nt in range(NT)]
+
+        def load_table(a):
+            nc.sync.dma_start(table[a][:], tab_words[a].rearrange("p t i -> p (t i)").bitcast(I32))
+
+        def load_w1(b, a, c0, c1):
+            nc.sync.dma_start(
+                w1_raw[b, a][:, :, c0:c1],
+                w1[a * PASS:(a + 1) * PASS, b * PASS + c0:b * PASS + c1].rearrange("(p j) c -> p j c", j=PACK))
+
+        nc.vector.memset(table_sc[:], 0)
+        nc.vector.memset(w2_sc[:], 0)
+        nc.sync.dma_start(gather_list[:], offs)
+        load_table(0)
+        for q in range(4):
+            nc.scalar.dma_start(table_sc[32 * q:32 * q + 4 * KP, :], tab_scales[:, 4 * q:4 * q + 4, :].bitcast(I32))
+        load_w1(0, 0, 0, PASS)
+        load_table(1)
+        load_w1(0, 1, 0, PASS)
+        for sb, vec in ((s0_sb, s0), (lo_sb, lo), (hi_sb, hi)):
+            nc.scalar.dma_start(sb[:], vec.rearrange("(b p t) -> p b t", p=P, t=PACK))
+        load_table(2)
+        load_w1(0, 2, 0, PASS)
+        load_w1(1, 0, 0, PASS)
+        load_w1(1, 1, 0, PASS)
+        load_w1(1, 2, 0, PASS // 2)
+        load_w1(1, 2, PASS // 2, PASS)
+        nc.sync.dma_start(w2_codes[:], w2_words.rearrange("a p c -> p a c").bitcast(I32))
+        for q in range(4):
+            nc.sync.dma_start(w2_sc[32 * q:32 * q + 4, :, :],
+                              w2_scales[:, 4 * q:4 * q + 4, :].rearrange("a r n -> r a n").bitcast(I32))
+        nc.sync.dma_start(scatter_list[:], offs2)
+        with nc.allow_non_contiguous_dma(reason="one bias value to a partition"):
+            nc.sync.dma_start(f0_sb[:], f0.rearrange("(n p) -> p n", p=P))
+        nc.sync.dma_start(wgo_sb[:], wgo)
+        for nt in range(NT):
+            nc.vector.memset(window[nt][:], 0.0)
+
+        def gather_words(a, j0, j1):
+            nc.vector.tensor_copy(v_codes[a][:, j0:j1], table[a][:].bitcast(U32).indirect(gather_list[:, j0 // 16:j1 // 16]))
+
+        def gather_scales(j0, j1):
+            nc.vector.tensor_copy(v_sc[:, j0:j1], table_sc[:].bitcast(U8).indirect(gather_list[:, j0 // 16:j1 // 16]))
+
+        def copy_on(engine, dst, src):
+            if engine == "v":
+                nc.vector.tensor_copy(dst, src)
+            else:
+                nc.scalar.copy(dst, src)
+
+        def quantize_w1(b, a, shares, pieces):
+            grouped = ring.tile([P, PACK, P, PACK], BF16, name="w1_grouped", align_bytes=64, bufs=3)
+            src = w1_raw[b, a][:].rearrange("p j (m t) -> p m j t", t=PACK)
+            dst = grouped[:].rearrange("p t m j -> p m j t")
+            for engine, m0, m1 in shares:
+                copy_on(engine, dst[:, m0:m1], src[:, m0:m1])
+            flat = grouped[:].rearrange("p t m j -> p (t m j)")
+            step = PASS // pieces
+            for c in range(0, PASS, step):
+                nc.vector.quantize_mx(out=w1_codes[b, a][:, c:c + step].bitcast(FP8X4), scales=w1_sc[b, a][:, c:c + step],
+                                      in_=flat[:, PACK * c:PACK * (c + step)])
+
+        def open_trial(j0, j1):
+            return [psum.tile([P, j1 - j0], F32, name="trial_acc", bufs=6) for t in range(PACK)]
+
+        def first_product(acc, b, a, j0, j1):
+            for t in range(PACK):
+                nc.tensor.matmul_mx(
+                    out=acc[t][:],
+                    lhsT=w1_codes[b, a][:, t * P:(t + 1) * P].bitcast(FP8X4),
+                    lhsT_scale=w1_sc[b, a][:, t * P:(t + 1) * P],
+                    rhs=v_codes[a][:, j0:j1].bitcast(FP8X4),
+                    rhs_scale=v_sc[4 * a:, j0:j1],
+                    start=(a == 0), stop=(a == KP - 1))
+
+        def make_h(acc, b, j0, j1, engine):
+            n = j1 - j0
+            planes = ring.tile([P, PACK, n], BF16, name="planes", bufs=3)
+            for t in range(PACK):
+                trial = ring.tile([P, n], F32, name="trial", bufs=6)
+                nc.scalar.activation(trial[:], acc[t][:], IDENT, bias=s0_sb[:, b, t:t + 1])
+                nc.vector.tensor_scalar(planes[:, t, :], trial[:], lo_sb[:, b, t:t + 1], hi_sb[:, b, t:t + 1], ALU.max, ALU.min)
+            grouped = ring.tile([P, n, PACK], BF16, name="h_grouped", align_bytes=64, bufs=2)
+            copy_on(engine, grouped[:].rearrange("p (c i) t -> p c t i", i=4), planes[:].rearrange("p t (c i) -> p c t i", i=4))
+            nc.vector.quantize_mx(out=h_codes[b][:, j0:j1].bitcast(FP8X4), scales=h_sc[b][:, j0:j1],
+                                  in_=grouped[:].rearrange("p n t -> p (n t)"))
+
+        def second_product(nt, j0, j1):
+            acc = psum.tile([P, j1 - j0], F32, name="force_acc", bufs=2)
+            width = 512 if j1 - j0 == 512 else 128
+            for g in range(j0, j1, width):
+                for b in range(HP):
+                    nc.tensor.matmul_mx(
+                        out=acc[:, g - j0:g - j0 + width],
+                        lhsT=w2_codes[:, b, :].bitcast(U8)[:, 2 * nt * P:2 * (nt + 1) * P].bitcast(FP4X4),
+                        lhsT_scale=w2_sc[:, b, :].bitcast(U8)[:, nt * P:(nt + 1) * P],
+                        rhs=h_codes[b][:, g:g + width].bitcast(FP8X4),
+                        rhs_scale=h_sc[b][:, g:g + width],
+                        start=(b == 0), stop=(b == HP - 1))
+            nc.scalar.activation(y_sb[nt][:, j0:j1], acc[:], IDENT, bias=f0_sb[:, nt:nt + 1])
+
+        def scatter(nt, j0, j1):
+            nc.vector.tensor_tensor(window[nt][:].indirect(scatter_list[:, j0 // 16:j1 // 16]), y_sb[nt][:, j0:j1], wgo_sb[:, j0:j1], ALU.mult)
+
+        def store(nt):
+            nc.sync.dma_start(out[nt * P:(nt + 1) * P, :], window[nt][:])
+
+        gather_words(0, 0, S)
+        gather_scales(0, S)
+        quantize_w1(0, 0, [("s", 0, 128)], 1)
+        gather_words(1, 0, S)
+        quantize_w1(0, 1, [("s", 0, 128)], 1)
+        acc00 = open_trial(0, 512)
+        first_product(acc00, 0, 0, 0, 512)
+        first_product(acc00, 0, 1, 0, 512)
+        gather_words(2, 0, 512)
+        gather_words(2, 512, S)
+        quantize_w1(0, 2, [("s", 0, 48), ("v", 48, 128)], 1)
+        first_product(acc00, 0, 2, 0, 512)
+        quantize_w1(1, 0, [("v", 0, 128)], 1)
+        make_h(acc00, 0, 0, 512, "v")
+        acc01 = open_trial(512, S)
+        for a in range(KP):
+            first_product(acc01, 0, a, 512, S)
+        quantize_w1(1, 1, [("s", 0, 128)], 1)
+        quantize_w1(1, 2, [("v", 0, 64), ("v", 64, 128)], 4)
+        make_h(acc01, 0, 512, S, "s")
+        for j0, j1, engine in ((0, 256, "v"), (256, 512, "s"), (512, S, "s")):
+            acc = open_trial(j0, j1)
+            for a in range(KP):
+                first_product(acc, 1, a, j0, j1)
+            make_h(acc, 1, j0, j1, engine)
+            for nt in range(NT):
+                second_product(nt, j0, j1)
+                if j0 == 0:
+                    scatter(nt, j0, j1)
+        for nt in range(2):
+            scatter(nt, 256, 512)
+        for nt in range(2):
+            scatter(nt, 512, S)
+            store(nt)
+        for nt in range(2, NT):
+            scatter(nt, 256, S)
+            store(nt)

@@ -66,8 +66,8 @@ def tile_list_yield_clipped_forces_kernel(tc, tab_words, tab_scales, w1, w2_word
                 w1_raw[b, a][:, :, c0:c1],
                 w1[a * PASS:(a + 1) * PASS, b * PASS + c0:b * PASS + c1].rearrange("(p j) c -> p j c", j=PACK))
 
-        nc.vector.memset(table_sc[:], 0)
-        nc.vector.memset(w2_sc[:], 0)
+        nc.gpsimd.memset(table_sc[:], 0)
+        nc.gpsimd.memset(w2_sc[:], 0)
         nc.sync.dma_start(gather_list[:], offs)
         load_table(0)
         for q in range(4):
@@ -92,7 +92,7 @@ def tile_list_yield_clipped_forces_kernel(tc, tab_words, tab_scales, w1, w2_word
             nc.sync.dma_start(f0_sb[:], f0.rearrange("(n p) -> p n", p=P))
         nc.sync.dma_start(wgo_sb[:], wgo)
         for nt in range(NT):
-            nc.vector.memset(window[nt][:], 0.0)
+            nc.gpsimd.memset(window[nt][:], 0.0)
 
         def gather_words(a, j0, j1):
             nc.vector.tensor_copy(v_codes[a][:, j0:j1], table[a][:].bitcast(U32).indirect(gather_list[:, j0 // 16:j1 // 16]))
@@ -131,15 +131,19 @@ def tile_list_yield_clipped_forces_kernel(tc, tab_words, tab_scales, w1, w2_word
                     rhs_scale=v_sc[4 * a:, j0:j1],
                     start=(a == 0), stop=(a == KP - 1))
 
-        def make_h(acc, b, j0, j1, engine):
-            n = j1 - j0
-            planes = ring.tile([P, PACK, n], BF16, name="planes", bufs=3)
+        def clip(acc, b):
+            n = acc[0].shape[1]
+            planes = ring.tile([P, PACK, n], BF16, name="planes", bufs=5)
             for t in range(PACK):
-                trial = ring.tile([P, n], F32, name="trial", bufs=6)
+                trial = ring.tile([P, n], F32, name="trial", bufs=8)
                 nc.scalar.activation(trial[:], acc[t][:], IDENT, bias=s0_sb[:, b, t:t + 1])
                 nc.vector.tensor_scalar(planes[:, t, :], trial[:], lo_sb[:, b, t:t + 1], hi_sb[:, b, t:t + 1], ALU.max, ALU.min)
-            grouped = ring.tile([P, n, PACK], BF16, name="h_grouped", align_bytes=64, bufs=2)
-            copy_on(engine, grouped[:].rearrange("p (c i) t -> p c t i", i=4), planes[:].rearrange("p t (c i) -> p c t i", i=4))
+            return planes
+
+        def quantize_h(planes, first, b, j0, j1, engine):
+            grouped = ring.tile([P, j1 - j0, PACK], BF16, name="h_grouped", align_bytes=64, bufs=3)
+            copy_on(engine, grouped[:].rearrange("p (c i) t -> p c t i", i=4),
+                    planes[:, :, j0 - first:j1 - first].rearrange("p t (c i) -> p c t i", i=4))
             nc.vector.quantize_mx(out=h_codes[b][:, j0:j1].bitcast(FP8X4), scales=h_sc[b][:, j0:j1],
                                   in_=grouped[:].rearrange("p n t -> p (n t)"))
 
@@ -173,30 +177,42 @@ def tile_list_yield_clipped_forces_kernel(tc, tab_words, tab_scales, w1, w2_word
         first_product(acc00, 0, 1, 0, 512)
         gather_words(2, 0, 512)
         gather_words(2, 512, S)
-        quantize_w1(0, 2, [("s", 0, 48), ("v", 48, 128)], 1)
+        quantize_w1(0, 2, [("s", 0, 48), ("v", 48, 128)], 2)
         first_product(acc00, 0, 2, 0, 512)
         quantize_w1(1, 0, [("v", 0, 128)], 1)
-        make_h(acc00, 0, 0, 512, "v")
+        planes00 = clip(acc00, 0)
         acc01 = open_trial(512, S)
         for a in range(KP):
             first_product(acc01, 0, a, 512, S)
-        quantize_w1(1, 1, [("s", 0, 128)], 1)
+        quantize_w1(1, 1, [("s", 0, 64), ("v", 64, 128)], 1)
         quantize_w1(1, 2, [("v", 0, 64), ("v", 64, 128)], 4)
-        make_h(acc01, 0, 512, S, "s")
-        for j0, j1, engine in ((0, 256, "v"), (256, 512, "s"), (512, S, "s")):
+        quantize_h(planes00, 0, 0, 0, 256, "v")
+        planes01 = clip(acc01, 0)
+        def second_half(j0, j1):
             acc = open_trial(j0, j1)
             for a in range(KP):
                 first_product(acc, 1, a, j0, j1)
-            make_h(acc, 1, j0, j1, engine)
-            for nt in range(NT):
-                second_product(nt, j0, j1)
-                if j0 == 0:
-                    scatter(nt, j0, j1)
-        for nt in range(2):
-            scatter(nt, 256, 512)
-        for nt in range(2):
-            scatter(nt, 512, S)
-            store(nt)
-        for nt in range(2, NT):
-            scatter(nt, 256, S)
+            return clip(acc, 1)
+
+        def forces(nt, j0, j1):
+            second_product(nt, j0, j1)
+            scatter(nt, j0, j1)
+
+        quantize_h(second_half(0, 256), 0, 1, 0, 256, "v")
+        forces(0, 0, 256)
+        planes11 = second_half(256, 512)
+        quantize_h(planes00, 0, 0, 256, 512, "s")
+        quantize_h(planes11, 256, 1, 256, 512, "s")
+        forces(1, 0, 256)
+        planes12 = second_half(512, S)
+        forces(2, 0, 256)
+        forces(3, 0, 256)
+        quantize_h(planes01, 512, 0, 512, S, "s")
+        forces(0, 256, 512)
+        forces(1, 256, 512)
+        quantize_h(planes12, 512, 1, 512, S, "s")
+        forces(2, 256, 512)
+        forces(3, 256, 512)
+        for nt in range(NT):
+            forces(nt, 512, S)
             store(nt)

@@ -74,10 +74,10 @@ def tile_list_yield_clipped_forces_kernel(tc, tab_words, tab_scales, w1, w2_word
             nc.scalar.dma_start(table_sc[32 * q:32 * q + 4 * KP, :], tab_scales[:, 4 * q:4 * q + 4, :].bitcast(I32))
         load_w1(0, 0, 0, PASS)
         load_table(1)
+        load_table(2)
         load_w1(0, 1, 0, PASS)
         for sb, vec in ((s0_sb, s0), (lo_sb, lo), (hi_sb, hi)):
             nc.scalar.dma_start(sb[:], vec.rearrange("(b p t) -> p b t", p=P, t=PACK))
-        load_table(2)
         load_w1(0, 2, 0, PASS)
         load_w1(1, 0, 0, PASS)
         load_w1(1, 1, 0, PASS)
@@ -106,49 +106,46 @@ def tile_list_yield_clipped_forces_kernel(tc, tab_words, tab_scales, w1, w2_word
             else:
                 nc.scalar.copy(dst, src)
 
-        def quantize_w1(b, a, shares, pieces):
-            grouped = ring.tile([P, PACK, P, PACK], BF16, name="w1_grouped", align_bytes=64, bufs=3)
+        def cast_w1(b, a, engine, m0, m1):
             src = w1_raw[b, a][:].rearrange("p j (m t) -> p m j t", t=PACK)
-            dst = grouped[:].rearrange("p t m j -> p m j t")
-            for engine, m0, m1 in shares:
-                copy_on(engine, dst[:, m0:m1], src[:, m0:m1])
-            flat = grouped[:].rearrange("p t m j -> p (t m j)")
-            step = PASS // pieces
-            for c in range(0, PASS, step):
-                nc.vector.quantize_mx(out=w1_codes[b, a][:, c:c + step].bitcast(FP8X4), scales=w1_sc[b, a][:, c:c + step],
-                                      in_=flat[:, PACK * c:PACK * (c + step)])
+            dst = w1_stage[b, a][:].rearrange("p t m j -> p m j t")
+            copy_on(engine, dst[:, m0:m1], src[:, m0:m1])
 
-        def open_trial(j0, j1):
-            return [psum.tile([P, j1 - j0], F32, name="trial_acc", bufs=6) for t in range(PACK)]
+        def quantize_w1(b, a, t0, t1):
+            flat = w1_stage[b, a][:].rearrange("p t m j -> p (t m j)")
+            nc.vector.quantize_mx(out=w1_codes[b, a][:, t0 * P:t1 * P].bitcast(FP8X4), scales=w1_sc[b, a][:, t0 * P:t1 * P],
+                                  in_=flat[:, PASS * t0:PASS * t1])
 
-        def first_product(acc, b, a, j0, j1):
+        def first_product(first_bank, b, a, j0, j1, start, stop):
             for t in range(PACK):
                 nc.tensor.matmul_mx(
-                    out=acc[t][:],
+                    out=bank[first_bank + t][:, :j1 - j0],
                     lhsT=w1_codes[b, a][:, t * P:(t + 1) * P].bitcast(FP8X4),
                     lhsT_scale=w1_sc[b, a][:, t * P:(t + 1) * P],
                     rhs=v_codes[a][:, j0:j1].bitcast(FP8X4),
                     rhs_scale=v_sc[4 * a:, j0:j1],
-                    start=(a == 0), stop=(a == KP - 1))
+                    start=start, stop=stop)
 
-        def clip(acc, b):
-            n = acc[0].shape[1]
-            planes = ring.tile([P, PACK, n], BF16, name="planes", bufs=5)
-            for t in range(PACK):
-                trial = ring.tile([P, n], F32, name="trial", bufs=8)
-                nc.scalar.activation(trial[:], acc[t][:], IDENT, bias=s0_sb[:, b, t:t + 1])
-                nc.vector.tensor_scalar(planes[:, t, :], trial[:], lo_sb[:, b, t:t + 1], hi_sb[:, b, t:t + 1], ALU.max, ALU.min)
-            return planes
+        def drain(first_bank, b, t, c0, c1, trial):
+            nc.scalar.activation(trial, bank[first_bank + t][:, c0:c1], IDENT, bias=s0_sb[:, b, t:t + 1])
 
-        def quantize_h(planes, first, b, j0, j1, engine):
-            grouped = ring.tile([P, j1 - j0, PACK], BF16, name="h_grouped", align_bytes=64, bufs=3)
-            copy_on(engine, grouped[:].rearrange("p (c i) t -> p c t i", i=4),
-                    planes[:, :, j0 - first:j1 - first].rearrange("p t (c i) -> p c t i", i=4))
+        def clip(planes, b, t, trial):
+            nc.vector.tensor_scalar(planes[:, t, :], trial, lo_sb[:, b, t:t + 1], hi_sb[:, b, t:t + 1], ALU.max, ALU.min)
+
+        def drain_clip(planes, first_bank, b, ts, c0, c1, trials):
+            for t in ts:
+                drain(first_bank, b, t, c0, c1, trials[t])
+                clip(planes, b, t, trials[t])
+
+        def weave(planes, c0, c1, grouped, engine):
+            copy_on(engine, grouped[:, :c1 - c0, :].rearrange("p (c i) t -> p c t i", i=4),
+                    planes[:, :, c0:c1].rearrange("p t (c i) -> p c t i", i=4))
+
+        def quantize_h(grouped, b, j0, j1):
             nc.vector.quantize_mx(out=h_codes[b][:, j0:j1].bitcast(FP8X4), scales=h_sc[b][:, j0:j1],
-                                  in_=grouped[:].rearrange("p n t -> p (n t)"))
+                                  in_=grouped[:, :j1 - j0, :].rearrange("p n t -> p (n t)"))
 
-        def second_product(nt, j0, j1):
-            acc = psum.tile([P, j1 - j0], F32, name="force_acc", bufs=2)
+        def second_product(acc, nt, j0, j1):
             width = 512 if j1 - j0 == 512 else 128
             for g in range(j0, j1, width):
                 for b in range(HP):
@@ -159,7 +156,7 @@ def tile_list_yield_clipped_forces_kernel(tc, tab_words, tab_scales, w1, w2_word
                         rhs=h_codes[b][:, g:g + width].bitcast(FP8X4),
                         rhs_scale=h_sc[b][:, g:g + width],
                         start=(b == 0), stop=(b == HP - 1))
-            nc.scalar.activation(y_sb[nt][:, j0:j1], acc[:], IDENT, bias=f0_sb[:, nt:nt + 1])
+            nc.scalar.activation(y_sb[nt][:, j0:j1], acc[:, :j1 - j0], IDENT, bias=f0_sb[:, nt:nt + 1])
 
         def scatter(nt, j0, j1):
             nc.vector.tensor_tensor(window[nt][:].indirect(scatter_list[:, j0 // 16:j1 // 16]), y_sb[nt][:, j0:j1], wgo_sb[:, j0:j1], ALU.mult)
@@ -167,52 +164,87 @@ def tile_list_yield_clipped_forces_kernel(tc, tab_words, tab_scales, w1, w2_word
         def store(nt):
             nc.sync.dma_start(out[nt * P:(nt + 1) * P, :], window[nt][:])
 
+        bank = [psum.tile([P, PASS], F32, name="bank%d" % i) for i in range(8)]
+        stage = [keep.tile([P, PACK, P, PACK], BF16, name="w1_stage%d" % i, align_bytes=64) for i in range(3)]
+        w1_stage = {(b, a): stage[a] for b in range(HP) for a in range(KP)}
+
+        woven = [stage[i][:].rearrange("p t m j -> p (t m) j") for i in range(3)]
+        planes = {key: keep.tile([P, PACK, width], BF16, name="planes_" + key)
+                  for key, width in (("00", 512), ("01", 512), ("10", 256), ("11", 256), ("12", 512))}
+        trial = [keep.tile([P, PASS], F32, name="trial%d" % i) for i in range(8)]
+        wide = [trial[t][:] for t in range(4)]
+        wide2 = [trial[4 + t][:] for t in range(4)]
+        half = [trial[4 + t][:, :256] for t in range(4)]
+        half2 = [trial[t][:, :256] for t in range(4)]
+        late = [w1_raw[1, 2][:, t, :] for t in range(4)]
+
         gather_words(0, 0, S)
         gather_scales(0, S)
-        quantize_w1(0, 0, [("s", 0, 128)], 1)
         gather_words(1, 0, S)
-        quantize_w1(0, 1, [("s", 0, 128)], 1)
-        acc00 = open_trial(0, 512)
-        first_product(acc00, 0, 0, 0, 512)
-        first_product(acc00, 0, 1, 0, 512)
-        gather_words(2, 0, 512)
-        gather_words(2, 512, S)
-        quantize_w1(0, 2, [("s", 0, 48), ("v", 48, 128)], 2)
-        first_product(acc00, 0, 2, 0, 512)
-        quantize_w1(1, 0, [("v", 0, 128)], 1)
-        planes00 = clip(acc00, 0)
-        acc01 = open_trial(512, S)
+        cast_w1(0, 0, "s", 0, 128)
+        quantize_w1(0, 0, 0, 4)
+        gather_words(2, 0, S)
+        first_product(0, 0, 0, 0, 512, True, False)
+        first_product(4, 0, 0, 512, S, True, False)
+        cast_w1(0, 1, "s", 0, 88)
+        cast_w1(0, 1, "v", 88, 128)
+        quantize_w1(0, 1, 0, 4)
+        first_product(0, 0, 1, 0, 512, False, False)
+        cast_w1(0, 2, "s", 0, 48)
+        cast_w1(0, 2, "v", 48, 128)
+        quantize_w1(0, 2, 0, 2)
+        quantize_w1(0, 2, 2, 4)
+        first_product(0, 0, 2, 0, 512, False, True)
+        first_product(4, 0, 2, 512, S, False, False)
+        first_product(4, 0, 1, 512, S, False, True)
+        cast_w1(1, 0, "v", 0, 128)
+        quantize_w1(1, 0, 0, 4)
+        drain_clip(planes["00"], 0, 0, range(4), 0, 512, wide)
+        first_product(0, 1, 0, 0, 512, True, False)
+        cast_w1(1, 1, "s", 0, 80)
+        cast_w1(1, 1, "v", 80, 128)
+        quantize_w1(1, 1, 0, 4)
+        first_product(0, 1, 1, 0, 512, False, False)
+        cast_w1(1, 2, "s", 0, 64)
+        cast_w1(1, 2, "v", 64, 128)
+        for t in range(PACK):
+            quantize_w1(1, 2, t, t + 1)
+        first_product(0, 1, 2, 0, 512, False, True)
+        weave(planes["00"], 0, 256, woven[1], "s")
+        quantize_h(woven[1], 0, 0, 256)
+        drain_clip(planes["10"], 0, 1, range(4), 0, 256, half)
+        weave(planes["10"], 0, 256, woven[0], "v")
+        quantize_h(woven[0], 1, 0, 256)
+        drain_clip(planes["01"], 4, 0, range(2), 0, 512, late)
+        second_product(bank[4], 0, 0, 256)
+        scatter(0, 0, 256)
+        second_product(bank[5], 1, 0, 256)
+        scatter(1, 0, 256)
+        drain_clip(planes["11"], 0, 1, range(4), 256, 512, half2)
+        drain_clip(planes["01"], 4, 0, range(2, 4), 0, 512, late)
+        weave(planes["00"], 256, 512, woven[0], "s")
+        quantize_h(woven[0], 0, 256, 512)
+        second_product(bank[6], 2, 0, 256)
+        scatter(2, 0, 256)
+        weave(planes["11"], 0, 256, woven[1], "s")
+        quantize_h(woven[1], 1, 256, 512)
+        second_product(bank[7], 3, 0, 256)
+        scatter(3, 0, 256)
         for a in range(KP):
-            first_product(acc01, 0, a, 512, S)
-        quantize_w1(1, 1, [("s", 0, 64), ("v", 64, 128)], 1)
-        quantize_w1(1, 2, [("v", 0, 64), ("v", 64, 128)], 4)
-        quantize_h(planes00, 0, 0, 0, 256, "v")
-        planes01 = clip(acc01, 0)
-        def second_half(j0, j1):
-            acc = open_trial(j0, j1)
-            for a in range(KP):
-                first_product(acc, 1, a, j0, j1)
-            return clip(acc, 1)
-
-        def forces(nt, j0, j1):
-            second_product(nt, j0, j1)
-            scatter(nt, j0, j1)
-
-        quantize_h(second_half(0, 256), 0, 1, 0, 256, "v")
-        forces(0, 0, 256)
-        planes11 = second_half(256, 512)
-        quantize_h(planes00, 0, 0, 256, 512, "s")
-        quantize_h(planes11, 256, 1, 256, 512, "s")
-        forces(1, 0, 256)
-        planes12 = second_half(512, S)
-        forces(2, 0, 256)
-        forces(3, 0, 256)
-        quantize_h(planes01, 512, 0, 512, S, "s")
-        forces(0, 256, 512)
-        forces(1, 256, 512)
-        quantize_h(planes12, 512, 1, 512, S, "s")
-        forces(2, 256, 512)
-        forces(3, 256, 512)
+            first_product(0, 1, a, 512, S, a == 0, a == KP - 1)
+        drain_clip(planes["12"], 0, 1, range(4), 0, 512, wide2)
+        for nt in range(2):
+            second_product(bank[4 + nt], nt, 256, 512)
+            scatter(nt, 256, 512)
+        weave(planes["01"], 0, 512, woven[0], "s")
+        quantize_h(woven[0], 0, 512, S)
+        second_product(bank[6], 2, 256, 512)
+        scatter(2, 256, 512)
+        weave(planes["12"], 0, 512, woven[1], "s")
+        quantize_h(woven[1], 1, 512, S)
+        second_product(bank[7], 3, 256, 512)
+        scatter(3, 256, 512)
         for nt in range(NT):
-            forces(nt, 512, S)
+            second_product(bank[4 + nt], nt, 512, S)
+            scatter(nt, 512, S)
             store(nt)

@@ -92,7 +92,7 @@ def tile_list_yield_clipped_forces_kernel(tc, tab_words, tab_scales, w1, w2_word
             nc.sync.dma_start(f0_sb[:], f0.rearrange("(n p) -> p n", p=P))
         nc.sync.dma_start(wgo_sb[:], wgo)
         for nt in range(NT):
-            nc.gpsimd.memset(window[nt][:], 0.0)
+            (nc.vector if nt < 2 else nc.gpsimd).memset(window[nt][:], 0.0)
 
         def gather_words(a, j0, j1):
             nc.vector.tensor_copy(v_codes[a][:, j0:j1], table[a][:].bitcast(U32).indirect(gather_list[:, j0 // 16:j1 // 16]))

@@ -22,6 +22,7 @@ PASS = P * PACK
 KP = K // PASS
 HP = H // PASS
 NT = N // P
+WHOLE = ()
 
 
 def tile_list_yield_clipped_forces_kernel(tc, tab_words, tab_scales, w1, w2_words, w2_scales,
@@ -38,12 +39,16 @@ def tile_list_yield_clipped_forces_kernel(tc, tab_words, tab_scales, w1, w2_word
         table_sc = keep.tile([P, T // 4], I32, name="table_sc")
         v_codes = [keep.tile([P, S], U32, name="v_codes%d" % a, align_bytes=64) for a in range(KP)]
         v_sc = keep.tile([P, S], U8, name="v_sc", align_bytes=64)
+        w1_rows = {a: keep.tile([P, PACK, H], F32, name="w1_rows%d" % a) for a in WHOLE}
         w1_raw = {}
         w1_codes = {}
         w1_sc = {}
         for b in range(HP):
             for a in range(KP):
-                w1_raw[b, a] = keep.tile([P, PACK, PASS], F32, name="w1_raw%d%d" % (b, a))
+                if a in WHOLE:
+                    w1_raw[b, a] = w1_rows[a][:, :, b * PASS:(b + 1) * PASS]
+                else:
+                    w1_raw[b, a] = keep.tile([P, PACK, PASS], F32, name="w1_raw%d%d" % (b, a), align_bytes=64)
                 w1_codes[b, a] = keep.tile([P, PASS], U32, name="w1_codes%d%d" % (b, a), align_bytes=64)
                 w1_sc[b, a] = keep.tile([P, PASS], U8, name="w1_sc%d%d" % (b, a), align_bytes=64)
         w2_codes = keep.tile([P, HP, N // 2], I32, name="w2_codes", align_bytes=64)
@@ -66,6 +71,9 @@ def tile_list_yield_clipped_forces_kernel(tc, tab_words, tab_scales, w1, w2_word
                 w1_raw[b, a][:, :, c0:c1],
                 w1[a * PASS:(a + 1) * PASS, b * PASS + c0:b * PASS + c1].rearrange("(p j) c -> p j c", j=PACK))
 
+        def load_rows(a):
+            nc.sync.dma_start(w1_rows[a][:], w1[a * PASS:(a + 1) * PASS, :].rearrange("(p j) c -> p j c", j=PACK))
+
         nc.gpsimd.memset(table_sc[:], 0)
         nc.gpsimd.memset(w2_sc[:], 0)
         nc.sync.dma_start(gather_list[:], offs)
@@ -75,14 +83,13 @@ def tile_list_yield_clipped_forces_kernel(tc, tab_words, tab_scales, w1, w2_word
         load_w1(0, 0, 0, PASS)
         load_table(1)
         load_table(2)
-        load_w1(0, 1, 0, PASS)
         for sb, vec in ((s0_sb, s0), (lo_sb, lo), (hi_sb, hi)):
             nc.scalar.dma_start(sb[:], vec.rearrange("(b p t) -> p b t", p=P, t=PACK))
+        load_w1(0, 1, 0, PASS)
         load_w1(0, 2, 0, PASS)
         load_w1(1, 0, 0, PASS)
         load_w1(1, 1, 0, PASS)
-        load_w1(1, 2, 0, PASS // 2)
-        load_w1(1, 2, PASS // 2, PASS)
+        load_w1(1, 2, 0, PASS)
         nc.sync.dma_start(w2_codes[:], w2_words.rearrange("a p c -> p a c").bitcast(I32))
         for q in range(4):
             nc.sync.dma_start(w2_sc[32 * q:32 * q + 4, :, :],
@@ -145,21 +152,21 @@ def tile_list_yield_clipped_forces_kernel(tc, tab_words, tab_scales, w1, w2_word
             nc.vector.quantize_mx(out=h_codes[b][:, j0:j1].bitcast(FP8X4), scales=h_sc[b][:, j0:j1],
                                   in_=grouped[:, :j1 - j0, :].rearrange("p n t -> p (n t)"))
 
-        def second_product(acc, nt, j0, j1):
+        def second_product(acc, nt, j0, j1, y):
             width = 512 if j1 - j0 == 512 else 128
-            for g in range(j0, j1, width):
-                for b in range(HP):
+            for b in range(HP):
+                for g in range(j0, j1, width):
                     nc.tensor.matmul_mx(
                         out=acc[:, g - j0:g - j0 + width],
                         lhsT=w2_codes[:, b, :].bitcast(U8)[:, 2 * nt * P:2 * (nt + 1) * P].bitcast(FP4X4),
                         lhsT_scale=w2_sc[:, b, :].bitcast(U8)[:, nt * P:(nt + 1) * P],
                         rhs=h_codes[b][:, g:g + width].bitcast(FP8X4),
                         rhs_scale=h_sc[b][:, g:g + width],
-                        start=(b == 0), stop=(b == HP - 1))
-            nc.scalar.activation(y_sb[nt][:, j0:j1], acc[:, :j1 - j0], IDENT, bias=f0_sb[:, nt:nt + 1])
+                        start=(b == 0 and g == j0), stop=(b == HP - 1 and g == j1 - width))
+            nc.scalar.activation(y, acc[:, :j1 - j0], IDENT, bias=f0_sb[:, nt:nt + 1])
 
-        def scatter(nt, j0, j1):
-            nc.vector.tensor_tensor(window[nt][:].indirect(scatter_list[:, j0 // 16:j1 // 16]), y_sb[nt][:, j0:j1], wgo_sb[:, j0:j1], ALU.mult)
+        def scatter(nt, j0, j1, y):
+            nc.vector.tensor_tensor(window[nt][:].indirect(scatter_list[:, j0 // 16:j1 // 16]), y, wgo_sb[:, j0:j1], ALU.mult)
 
         def store(nt):
             nc.sync.dma_start(out[nt * P:(nt + 1) * P, :], window[nt][:])
@@ -177,6 +184,11 @@ def tile_list_yield_clipped_forces_kernel(tc, tab_words, tab_scales, w1, w2_word
         half = [trial[4 + t][:, :256] for t in range(4)]
         half2 = [trial[t][:, :256] for t in range(4)]
         late = [w1_raw[1, 2][:, t, :] for t in range(4)]
+
+        def forces(nt, j0, j1, y=None):
+            y = y_sb[nt][:, j0:j1] if y is None else y
+            second_product(bank[nt], nt, j0, j1, y)
+            scatter(nt, j0, j1, y)
 
         gather_words(0, 0, S)
         gather_scales(0, S)
@@ -199,52 +211,55 @@ def tile_list_yield_clipped_forces_kernel(tc, tab_words, tab_scales, w1, w2_word
         first_product(4, 0, 1, 512, S, False, True)
         cast_w1(1, 0, "v", 0, 128)
         quantize_w1(1, 0, 0, 4)
-        drain_clip(planes["00"], 0, 0, range(4), 0, 512, wide)
-        first_product(0, 1, 0, 0, 512, True, False)
-        cast_w1(1, 1, "s", 0, 80)
-        cast_w1(1, 1, "v", 80, 128)
+        cast_w1(1, 1, "v", 0, 128)
         quantize_w1(1, 1, 0, 4)
-        first_product(0, 1, 1, 0, 512, False, False)
-        cast_w1(1, 2, "s", 0, 64)
-        cast_w1(1, 2, "v", 64, 128)
+        cast_w1(1, 2, "s", 0, 48)
+        cast_w1(1, 2, "v", 48, 128)
         for t in range(PACK):
             quantize_w1(1, 2, t, t + 1)
-        first_product(0, 1, 2, 0, 512, False, True)
-        weave(planes["00"], 0, 256, woven[1], "s")
-        quantize_h(woven[1], 0, 0, 256)
-        drain_clip(planes["10"], 0, 1, range(4), 0, 256, half)
-        weave(planes["10"], 0, 256, woven[0], "v")
-        quantize_h(woven[0], 1, 0, 256)
-        drain_clip(planes["01"], 4, 0, range(2), 0, 512, late)
-        second_product(bank[4], 0, 0, 256)
-        scatter(0, 0, 256)
-        second_product(bank[5], 1, 0, 256)
-        scatter(1, 0, 256)
-        drain_clip(planes["11"], 0, 1, range(4), 256, 512, half2)
-        drain_clip(planes["01"], 4, 0, range(2, 4), 0, 512, late)
-        weave(planes["00"], 256, 512, woven[0], "s")
-        quantize_h(woven[0], 0, 256, 512)
-        second_product(bank[6], 2, 0, 256)
-        scatter(2, 0, 256)
-        weave(planes["11"], 0, 256, woven[1], "s")
-        quantize_h(woven[1], 1, 256, 512)
-        second_product(bank[7], 3, 0, 256)
-        scatter(3, 0, 256)
+        drain_clip(planes["00"], 0, 0, range(4), 0, 512, wide)
         for a in range(KP):
-            first_product(0, 1, a, 512, S, a == 0, a == KP - 1)
-        drain_clip(planes["12"], 0, 1, range(4), 0, 512, wide2)
-        for nt in range(2):
-            second_product(bank[4 + nt], nt, 256, 512)
-            scatter(nt, 256, 512)
-        weave(planes["01"], 0, 512, woven[0], "s")
-        quantize_h(woven[0], 0, 512, S)
-        second_product(bank[6], 2, 256, 512)
-        scatter(2, 256, 512)
-        weave(planes["12"], 0, 512, woven[1], "s")
-        quantize_h(woven[1], 1, 512, S)
-        second_product(bank[7], 3, 256, 512)
-        scatter(3, 256, 512)
+            first_product(0, 1, a, 0, 256, a == 0, a == KP - 1)
+        for t in range(PACK):
+            drain(4, 0, t, 0, 512, wide2[t])
+        for t in range(3):
+            clip(planes["01"], 0, t, wide2[t])
+        for t in range(PACK):
+            drain(0, 1, t, 0, 256, late[t][:, :256])
+        weave(planes["00"], 0, 256, woven[0], "s")
+        for t in range(PACK):
+            clip(planes["10"], 1, t, late[t][:, :256])
+        weave(planes["10"], 0, 256, woven[1], "v")
+        quantize_h(woven[1], 1, 0, 256)
+        for t in range(3, PACK):
+            clip(planes["01"], 0, t, wide2[t])
+        quantize_h(woven[0], 0, 0, 256)
+        for a in (0, 2, 1):
+            first_product(4, 1, a, 256, 768, a == 0, a == 1)
+        spare = late[2].bitcast(BF16).rearrange("p (n t) -> p n t", t=PACK)
+        weave(planes["00"], 256, 512, spare, "s")
+        quantize_h(spare, 0, 256, 512)
+        drain_clip(planes["12"], 4, 1, range(2), 0, 512, wide)
+        forces(0, 0, 256, stage[2][:].rearrange("p t m j -> p (t m j)").bitcast(F32)[:, :256])
+        forces(1, 0, 256)
+        drain_clip(planes["12"], 4, 1, range(2, 4), 0, 512, wide)
+        forces(2, 0, 256)
+        weave(planes["01"], 0, 512, woven[2], "s")
+        quantize_h(woven[2], 0, 512, S)
+        weave(planes["12"], 0, 256, woven[0], "s")
+        quantize_h(woven[0], 1, 256, 512)
+        forces(3, 0, 256, wide[3][:, :256])
+        for a in range(KP):
+            first_product(4, 1, a, 768, S, a == 0, a == KP - 1)
+        drain_clip(planes["11"], 4, 1, range(4), 0, 256, half)
+        forces(0, 256, 512)
+        weave(planes["12"], 256, 512, woven[1], "s")
+        quantize_h(woven[1], 1, 512, 768)
+        forces(1, 256, 512)
+        weave(planes["11"], 0, 256, woven[0], "s")
+        quantize_h(woven[0], 1, 768, S)
+        forces(2, 256, 512, half[3])
+        forces(3, 256, 512)
         for nt in range(NT):
-            second_product(bank[4 + nt], nt, 512, S)
-            scatter(nt, 512, S)
+            forces(nt, 512, S)
             store(nt)

@@ -1,6 +1,7 @@
 from contextlib import ExitStack
 
 import concourse.mybir as mybir
+from concourse.masks import make_identity
 
 K, H, N, T, S, T2 = 1536, 1024, 512, 2048, 1024, 2048
 FLOPS = 2 * K * H * S + 2 * H * N * S
@@ -53,9 +54,9 @@ def tile_list_yield_clipped_forces_kernel(tc, tab_words, tab_scales, w1, w2_word
                 w1_sc[b, a] = keep.tile([P, PASS], U8, name="w1_sc%d%d" % (b, a), align_bytes=64)
         w2_codes = keep.tile([P, HP, N // 2], I32, name="w2_codes", align_bytes=64)
         w2_sc = keep.tile([P, HP, N // 4], I32, name="w2_sc", align_bytes=64)
-        s0_sb = keep.tile([P, HP, PACK], F32, name="s0_sb")
-        lo_sb = keep.tile([P, HP, PACK], F32, name="lo_sb")
-        hi_sb = keep.tile([P, HP, PACK], F32, name="hi_sb")
+        vec_rows = keep.tile([P, PASS], F32, name="vec_rows")
+        identity = keep.tile([P, P], F32, name="identity")
+        row_consts = keep.tile([P, PACK, 3 * HP], F32, name="row_consts")
         f0_sb = keep.tile([P, NT], F32, name="f0_sb")
         wgo_sb = keep.tile([P, S], F32, name="wgo_sb")
         h_codes = [keep.tile([P, S], U32, name="h_codes%d" % b, align_bytes=64) for b in range(HP)]
@@ -75,7 +76,9 @@ def tile_list_yield_clipped_forces_kernel(tc, tab_words, tab_scales, w1, w2_word
             nc.sync.dma_start(w1_rows[a][:], w1[a * PASS:(a + 1) * PASS, :].rearrange("(p j) c -> p j c", j=PACK))
 
         nc.gpsimd.memset(table_sc[:], 0)
+        nc.vector.memset(vec_rows[:], 0.0)
         nc.gpsimd.memset(w2_sc[:], 0)
+        make_identity(nc, identity[:])
         nc.sync.dma_start(gather_list[:], offs)
         load_table(0)
         for q in range(4):
@@ -83,8 +86,9 @@ def tile_list_yield_clipped_forces_kernel(tc, tab_words, tab_scales, w1, w2_word
         load_w1(0, 0, 0, PASS)
         load_table(1)
         load_table(2)
-        for sb, vec in ((s0_sb, s0), (lo_sb, lo), (hi_sb, hi)):
-            nc.scalar.dma_start(sb[:], vec.rearrange("(b p t) -> p b t", p=P, t=PACK))
+        for i, vec in enumerate((s0, lo, hi)):
+            nc.scalar.dma_start(vec_rows[HP * i:HP * (i + 1), :], vec.rearrange("(b c) -> b c", b=HP))
+        nc.scalar.dma_start(vec_rows[8:8 + NT, :P], f0.rearrange("(n p) -> n p", p=P))
         load_w1(0, 1, 0, PASS)
         load_w1(0, 2, 0, PASS)
         load_w1(1, 0, 0, PASS)
@@ -95,8 +99,6 @@ def tile_list_yield_clipped_forces_kernel(tc, tab_words, tab_scales, w1, w2_word
             nc.sync.dma_start(w2_sc[32 * q:32 * q + 4, :, :],
                               w2_scales[:, 4 * q:4 * q + 4, :].rearrange("a r n -> r a n").bitcast(I32))
         nc.sync.dma_start(scatter_list[:], offs2)
-        with nc.allow_non_contiguous_dma(reason="one bias value to a partition"):
-            nc.sync.dma_start(f0_sb[:], f0.rearrange("(n p) -> p n", p=P))
         nc.sync.dma_start(wgo_sb[:], wgo)
         for nt in range(NT):
             (nc.vector if nt < 2 else nc.gpsimd).memset(window[nt][:], 0.0)
@@ -134,10 +136,10 @@ def tile_list_yield_clipped_forces_kernel(tc, tab_words, tab_scales, w1, w2_word
                     start=start, stop=stop)
 
         def drain(first_bank, b, t, c0, c1, trial):
-            nc.scalar.activation(trial, bank[first_bank + t][:, c0:c1], IDENT, bias=s0_sb[:, b, t:t + 1])
+            nc.scalar.activation(trial, bank[first_bank + t][:, c0:c1], IDENT, bias=row_consts[:, t, b:b + 1])
 
         def clip(planes, b, t, trial):
-            nc.vector.tensor_scalar(planes[:, t, :], trial, lo_sb[:, b, t:t + 1], hi_sb[:, b, t:t + 1], ALU.max, ALU.min)
+            nc.vector.tensor_scalar(planes[:, t, :], trial, row_consts[:, t, HP + b:HP + b + 1], row_consts[:, t, 2 * HP + b:2 * HP + b + 1], ALU.max, ALU.min)
 
         def drain_clip(planes, first_bank, b, ts, c0, c1, trials):
             for t in ts:
@@ -190,6 +192,11 @@ def tile_list_yield_clipped_forces_kernel(tc, tab_words, tab_scales, w1, w2_word
             second_product(bank[nt], nt, j0, j1, y)
             scatter(nt, j0, j1, y)
 
+        for t in range(PACK):
+            nc.tensor.transpose(bank[0][:, t * P:(t + 1) * P], vec_rows[:, t:PASS:PACK], identity[:])
+        nc.tensor.transpose(bank[1][:, :P], vec_rows[:, :P], identity[:])
+        nc.scalar.copy(row_consts[:], bank[0][:].rearrange("p (t r) -> p t r", t=PACK)[:, :, :3 * HP])
+        nc.scalar.copy(f0_sb[:], bank[1][:, 8:8 + NT])
         gather_words(0, 0, S)
         gather_scales(0, S)
         gather_words(1, 0, S)

@@ -54,9 +54,9 @@ def tile_list_yield_clipped_forces_kernel(tc, tab_words, tab_scales, w1, w2_word
                 w1_sc[b, a] = keep.tile([P, PASS], U8, name="w1_sc%d%d" % (b, a), align_bytes=64)
         w2_codes = keep.tile([P, HP, N // 2], I32, name="w2_codes", align_bytes=64)
         w2_sc = keep.tile([P, HP, N // 4], I32, name="w2_sc", align_bytes=64)
-        vec_rows = keep.tile([P, PASS], F32, name="vec_rows")
+        vec_rows = keep.tile([P, H], F32, name="vec_rows")
         identity = keep.tile([P, P], F32, name="identity")
-        row_consts = keep.tile([P, PACK, 3 * HP], F32, name="row_consts")
+        row_consts = keep.tile([P, HP, PACK, 3], F32, name="row_consts")
         f0_sb = keep.tile([P, NT], F32, name="f0_sb")
         wgo_sb = keep.tile([P, S], F32, name="wgo_sb")
         h_codes = [keep.tile([P, S], U32, name="h_codes%d" % b, align_bytes=64) for b in range(HP)]
@@ -86,9 +86,8 @@ def tile_list_yield_clipped_forces_kernel(tc, tab_words, tab_scales, w1, w2_word
         load_w1(0, 0, 0, PASS)
         load_table(1)
         load_table(2)
-        for i, vec in enumerate((s0, lo, hi)):
-            nc.scalar.dma_start(vec_rows[HP * i:HP * (i + 1), :], vec.rearrange("(b c) -> b c", b=HP))
-        nc.scalar.dma_start(vec_rows[8:8 + NT, :P], f0.rearrange("(n p) -> n p", p=P))
+        for i, vec in enumerate((s0, lo, hi, f0)):
+            nc.scalar.dma_start(vec_rows[i:i + 1, :vec.shape[0]], vec.rearrange("(o c) -> o c", o=1))
         load_w1(0, 1, 0, PASS)
         load_w1(0, 2, 0, PASS)
         load_w1(1, 0, 0, PASS)
@@ -136,10 +135,10 @@ def tile_list_yield_clipped_forces_kernel(tc, tab_words, tab_scales, w1, w2_word
                     start=start, stop=stop)
 
         def drain(first_bank, b, t, c0, c1, trial):
-            nc.scalar.activation(trial, bank[first_bank + t][:, c0:c1], IDENT, bias=row_consts[:, t, b:b + 1])
+            nc.scalar.activation(trial, bank[first_bank + t][:, c0:c1], IDENT, bias=row_consts[:, b, t, 0:1])
 
         def clip(planes, b, t, trial):
-            nc.vector.tensor_scalar(planes[:, t, :], trial, row_consts[:, t, HP + b:HP + b + 1], row_consts[:, t, 2 * HP + b:2 * HP + b + 1], ALU.max, ALU.min)
+            nc.vector.tensor_scalar(planes[:, t, :], trial, row_consts[:, b, t, 1:2], row_consts[:, b, t, 2:3], ALU.max, ALU.min)
 
         def drain_clip(planes, first_bank, b, ts, c0, c1, trials):
             for t in ts:
@@ -192,11 +191,13 @@ def tile_list_yield_clipped_forces_kernel(tc, tab_words, tab_scales, w1, w2_word
             second_product(bank[nt], nt, j0, j1, y)
             scatter(nt, j0, j1, y)
 
-        for t in range(PACK):
-            nc.tensor.transpose(bank[0][:, t * P:(t + 1) * P], vec_rows[:, t:PASS:PACK], identity[:])
-        nc.tensor.transpose(bank[1][:, :P], vec_rows[:, :P], identity[:])
-        nc.scalar.copy(row_consts[:], bank[0][:].rearrange("p (t r) -> p t r", t=PACK)[:, :, :3 * HP])
-        nc.scalar.copy(f0_sb[:], bank[1][:, 8:8 + NT])
+        for b in range(HP):
+            for t in range(PACK):
+                nc.tensor.transpose(bank[b][:, t * P:(t + 1) * P], vec_rows[:, b * PASS + t:(b + 1) * PASS:PACK], identity[:])
+            nc.scalar.copy(row_consts[:, b], bank[b][:].rearrange("p (t r) -> p t r", t=PACK)[:, :, :3])
+        for nt in range(NT):
+            nc.tensor.transpose(bank[HP][:, nt * P:(nt + 1) * P], vec_rows[:, nt * P:(nt + 1) * P], identity[:])
+        nc.scalar.copy(f0_sb[:], bank[HP][:].rearrange("p (n r) -> p n r", n=NT)[:, :, 3])
         gather_words(0, 0, S)
         gather_scales(0, S)
         gather_words(1, 0, S)
@@ -218,18 +219,18 @@ def tile_list_yield_clipped_forces_kernel(tc, tab_words, tab_scales, w1, w2_word
         first_product(4, 0, 1, 512, S, False, True)
         cast_w1(1, 0, "v", 0, 128)
         quantize_w1(1, 0, 0, 4)
+        drain_clip(planes["00"], 0, 0, range(4), 0, 512, wide)
         cast_w1(1, 1, "v", 0, 128)
         quantize_w1(1, 1, 0, 4)
-        cast_w1(1, 2, "s", 0, 48)
-        cast_w1(1, 2, "v", 48, 128)
+        cast_w1(1, 2, "s", 0, 24)
+        cast_w1(1, 2, "v", 24, 128)
         for t in range(PACK):
             quantize_w1(1, 2, t, t + 1)
-        drain_clip(planes["00"], 0, 0, range(4), 0, 512, wide)
         for a in range(KP):
             first_product(0, 1, a, 0, 256, a == 0, a == KP - 1)
         for t in range(PACK):
             drain(4, 0, t, 0, 512, wide2[t])
-        for t in range(3):
+        for t in range(4):
             clip(planes["01"], 0, t, wide2[t])
         for t in range(PACK):
             drain(0, 1, t, 0, 256, late[t][:, :256])
@@ -238,12 +239,12 @@ def tile_list_yield_clipped_forces_kernel(tc, tab_words, tab_scales, w1, w2_word
             clip(planes["10"], 1, t, late[t][:, :256])
         weave(planes["10"], 0, 256, woven[1], "v")
         quantize_h(woven[1], 1, 0, 256)
-        for t in range(3, PACK):
+        for t in range(4, PACK):
             clip(planes["01"], 0, t, wide2[t])
         quantize_h(woven[0], 0, 0, 256)
         for a in (0, 2, 1):
             first_product(4, 1, a, 256, 768, a == 0, a == 1)
-        spare = late[2].bitcast(BF16).rearrange("p (n t) -> p n t", t=PACK)
+        spare = w1_raw[1, 1][:, 0, :].bitcast(BF16).rearrange("p (n t) -> p n t", t=PACK)
         weave(planes["00"], 256, 512, spare, "s")
         quantize_h(spare, 0, 256, 512)
         drain_clip(planes["12"], 4, 1, range(2), 0, 512, wide)

@@ -54,9 +54,9 @@ def tile_list_yield_clipped_forces_kernel(tc, tab_words, tab_scales, w1, w2_word
                 w1_sc[b, a] = keep.tile([P, PASS], U8, name="w1_sc%d%d" % (b, a), align_bytes=64)
         w2_codes = keep.tile([P, HP, N // 2], I32, name="w2_codes", align_bytes=64)
         w2_sc = keep.tile([P, HP, N // 4], I32, name="w2_sc", align_bytes=64)
-        vec_rows = keep.tile([P, H], F32, name="vec_rows")
+        vec_rows = keep.tile([P, PASS], F32, name="vec_rows")
         identity = keep.tile([P, P], F32, name="identity")
-        row_consts = keep.tile([P, HP, PACK, 3], F32, name="row_consts")
+        row_consts = keep.tile([P, PACK, 3 * HP], F32, name="row_consts")
         f0_sb = keep.tile([P, NT], F32, name="f0_sb")
         wgo_sb = keep.tile([P, S], F32, name="wgo_sb")
         h_codes = [keep.tile([P, S], U32, name="h_codes%d" % b, align_bytes=64) for b in range(HP)]
@@ -86,8 +86,9 @@ def tile_list_yield_clipped_forces_kernel(tc, tab_words, tab_scales, w1, w2_word
         load_w1(0, 0, 0, PASS)
         load_table(1)
         load_table(2)
-        for i, vec in enumerate((s0, lo, hi, f0)):
-            nc.scalar.dma_start(vec_rows[i:i + 1, :vec.shape[0]], vec.rearrange("(o c) -> o c", o=1))
+        for i, vec in enumerate((s0, lo, hi)):
+            nc.scalar.dma_start(vec_rows[HP * i:HP * (i + 1), :], vec.rearrange("(b c) -> b c", b=HP))
+        nc.scalar.dma_start(vec_rows[8:8 + NT, :P], f0.rearrange("(n p) -> n p", p=P))
         load_w1(0, 1, 0, PASS)
         load_w1(0, 2, 0, PASS)
         load_w1(1, 0, 0, PASS)
@@ -135,10 +136,10 @@ def tile_list_yield_clipped_forces_kernel(tc, tab_words, tab_scales, w1, w2_word
                     start=start, stop=stop)
 
         def drain(first_bank, b, t, c0, c1, trial):
-            nc.scalar.activation(trial, bank[first_bank + t][:, c0:c1], IDENT, bias=row_consts[:, b, t, 0:1])
+            nc.scalar.activation(trial, bank[first_bank + t][:, c0:c1], IDENT, bias=row_consts[:, t, b:b + 1])
 
         def clip(planes, b, t, trial):
-            nc.vector.tensor_scalar(planes[:, t, :], trial, row_consts[:, b, t, 1:2], row_consts[:, b, t, 2:3], ALU.max, ALU.min)
+            nc.vector.tensor_scalar(planes[:, t, :], trial, row_consts[:, t, HP + b:HP + b + 1], row_consts[:, t, 2 * HP + b:2 * HP + b + 1], ALU.max, ALU.min)
 
         def drain_clip(planes, first_bank, b, ts, c0, c1, trials):
             for t in ts:
@@ -191,13 +192,11 @@ def tile_list_yield_clipped_forces_kernel(tc, tab_words, tab_scales, w1, w2_word
             second_product(bank[nt], nt, j0, j1, y)
             scatter(nt, j0, j1, y)
 
-        for b in range(HP):
-            for t in range(PACK):
-                nc.tensor.transpose(bank[b][:, t * P:(t + 1) * P], vec_rows[:, b * PASS + t:(b + 1) * PASS:PACK], identity[:])
-            nc.scalar.copy(row_consts[:, b], bank[b][:].rearrange("p (t r) -> p t r", t=PACK)[:, :, :3])
-        for nt in range(NT):
-            nc.tensor.transpose(bank[HP][:, nt * P:(nt + 1) * P], vec_rows[:, nt * P:(nt + 1) * P], identity[:])
-        nc.scalar.copy(f0_sb[:], bank[HP][:].rearrange("p (n r) -> p n r", n=NT)[:, :, 3])
+        for t in range(PACK):
+            nc.tensor.transpose(bank[0][:, t * P:(t + 1) * P], vec_rows[:, t:PASS:PACK], identity[:])
+        nc.tensor.transpose(bank[1][:, :P], vec_rows[:, :P], identity[:])
+        nc.scalar.copy(row_consts[:], bank[0][:].rearrange("p (t r) -> p t r", t=PACK)[:, :, :3 * HP])
+        nc.scalar.copy(f0_sb[:], bank[1][:, 8:8 + NT])
         gather_words(0, 0, S)
         gather_scales(0, S)
         gather_words(1, 0, S)

@@ -24,6 +24,7 @@ KP = K // PASS
 HP = H // PASS
 NT = N // P
 WHOLE = ()
+HALVED = ((1, 0), (1, 2))
 
 
 def tile_list_yield_clipped_forces_kernel(tc, tab_words, tab_scales, w1, w2_words, w2_scales,
@@ -48,10 +49,15 @@ def tile_list_yield_clipped_forces_kernel(tc, tab_words, tab_scales, w1, w2_word
             for a in range(KP):
                 if a in WHOLE:
                     w1_raw[b, a] = w1_rows[a][:, :, b * PASS:(b + 1) * PASS]
-                else:
+                elif (b, a) in HALVED:
+                    w1_raw[b, a] = [keep.tile([P, PACK, PASS // 2], F32, name="w1_raw%d%d_%d" % (b, a, h), align_bytes=64)
+                                    for h in range(2)]
+                elif (b, a) != (1, 1):
                     w1_raw[b, a] = keep.tile([P, PACK, PASS], F32, name="w1_raw%d%d" % (b, a), align_bytes=64)
                 w1_codes[b, a] = keep.tile([P, PASS], U32, name="w1_codes%d%d" % (b, a), align_bytes=64)
                 w1_sc[b, a] = keep.tile([P, PASS], U8, name="w1_sc%d%d" % (b, a), align_bytes=64)
+        raw11 = keep.tile([P, 512 + PACK * PASS], F32, name="raw11", align_bytes=64)
+        w1_raw[1, 1] = raw11[:, 512:].rearrange("p (j c) -> p j c", j=PACK)
         w2_codes = keep.tile([P, HP, N // 2], I32, name="w2_codes", align_bytes=64)
         w2_sc = keep.tile([P, HP, N // 4], I32, name="w2_sc", align_bytes=64)
         vec_rows = keep.tile([P, PASS], F32, name="vec_rows")
@@ -68,8 +74,9 @@ def tile_list_yield_clipped_forces_kernel(tc, tab_words, tab_scales, w1, w2_word
             nc.sync.dma_start(table[a][:], tab_words[a].rearrange("p t i -> p (t i)").bitcast(I32))
 
         def load_w1(b, a, c0, c1):
+            dst = w1_raw[b, a][2 * c0 // PASS][:] if (b, a) in HALVED else w1_raw[b, a][:, :, c0:c1]
             nc.sync.dma_start(
-                w1_raw[b, a][:, :, c0:c1],
+                dst,
                 w1[a * PASS:(a + 1) * PASS, b * PASS + c0:b * PASS + c1].rearrange("(p j) c -> p j c", j=PACK))
 
         def load_rows(a):
@@ -91,9 +98,11 @@ def tile_list_yield_clipped_forces_kernel(tc, tab_words, tab_scales, w1, w2_word
         nc.scalar.dma_start(vec_rows[8:8 + NT, :P], f0.rearrange("(n p) -> n p", p=P))
         load_w1(0, 1, 0, PASS)
         load_w1(0, 2, 0, PASS)
-        load_w1(1, 0, 0, PASS)
+        load_w1(1, 0, 0, PASS // 2)
+        load_w1(1, 0, PASS // 2, PASS)
         load_w1(1, 1, 0, PASS)
-        load_w1(1, 2, 0, PASS)
+        load_w1(1, 2, 0, PASS // 2)
+        load_w1(1, 2, PASS // 2, PASS)
         nc.sync.dma_start(w2_codes[:], w2_words.rearrange("a p c -> p a c").bitcast(I32))
         for q in range(4):
             nc.sync.dma_start(w2_sc[32 * q:32 * q + 4, :, :],
@@ -116,9 +125,11 @@ def tile_list_yield_clipped_forces_kernel(tc, tab_words, tab_scales, w1, w2_word
                 nc.scalar.copy(dst, src)
 
         def cast_w1(b, a, engine, m0, m1):
-            src = w1_raw[b, a][:].rearrange("p j (m t) -> p m j t", t=PACK)
+            first = 64 * (m0 // 64) if (b, a) in HALVED else 0
+            raw = w1_raw[b, a][m0 // 64] if (b, a) in HALVED else w1_raw[b, a]
+            src = raw[:].rearrange("p j (m t) -> p m j t", t=PACK)
             dst = w1_stage[b, a][:].rearrange("p t m j -> p m j t")
-            copy_on(engine, dst[:, m0:m1], src[:, m0:m1])
+            copy_on(engine, dst[:, m0:m1], src[:, m0 - first:m1 - first])
 
         def quantize_w1(b, a, t0, t1):
             flat = w1_stage[b, a][:].rearrange("p t m j -> p (t m j)")
@@ -179,13 +190,14 @@ def tile_list_yield_clipped_forces_kernel(tc, tab_words, tab_scales, w1, w2_word
 
         woven = [stage[i][:].rearrange("p t m j -> p (t m) j") for i in range(3)]
         planes = {key: keep.tile([P, PACK, width], BF16, name="planes_" + key)
-                  for key, width in (("00", 512), ("01", 512), ("10", 256), ("11", 256), ("12", 512))}
+                  for key, width in (("10", 256), ("11", 256), ("12", 512))}
         trial = [keep.tile([P, PASS], F32, name="trial%d" % i) for i in range(8)]
+        late_all = keep.tile([P, PACK * 256], F32, name="late", align_bytes=64)
+        late = [late_all[:, 256 * t:256 * (t + 1)] for t in range(PACK)]
+        first_plane = raw11[:, :1024].bitcast(BF16).rearrange("p (t c) -> p t c", t=PACK)
         wide = [trial[t][:] for t in range(4)]
         wide2 = [trial[4 + t][:] for t in range(4)]
         half = [trial[4 + t][:, :256] for t in range(4)]
-        half2 = [trial[t][:, :256] for t in range(4)]
-        late = [w1_raw[1, 2][:, t, :] for t in range(4)]
 
         def forces(nt, j0, j1, y=None):
             y = y_sb[nt][:, j0:j1] if y is None else y
@@ -205,8 +217,8 @@ def tile_list_yield_clipped_forces_kernel(tc, tab_words, tab_scales, w1, w2_word
         gather_words(2, 0, S)
         first_product(0, 0, 0, 0, 512, True, False)
         first_product(4, 0, 0, 512, S, True, False)
-        cast_w1(0, 1, "s", 0, 88)
-        cast_w1(0, 1, "v", 88, 128)
+        cast_w1(0, 1, "s", 0, 72)
+        cast_w1(0, 1, "v", 72, 128)
         quantize_w1(0, 1, 0, 4)
         first_product(0, 0, 1, 0, 512, False, False)
         cast_w1(0, 2, "s", 0, 48)
@@ -216,57 +228,58 @@ def tile_list_yield_clipped_forces_kernel(tc, tab_words, tab_scales, w1, w2_word
         first_product(0, 0, 2, 0, 512, False, True)
         first_product(4, 0, 2, 512, S, False, False)
         first_product(4, 0, 1, 512, S, False, True)
-        cast_w1(1, 0, "v", 0, 128)
+        cast_w1(1, 0, "s", 0, 64)
+        cast_w1(1, 0, "v", 64, 128)
         quantize_w1(1, 0, 0, 4)
-        drain_clip(planes["00"], 0, 0, range(4), 0, 512, wide)
         cast_w1(1, 1, "v", 0, 128)
         quantize_w1(1, 1, 0, 4)
-        cast_w1(1, 2, "s", 0, 24)
-        cast_w1(1, 2, "v", 24, 128)
-        for t in range(PACK):
-            quantize_w1(1, 2, t, t + 1)
+        cast_w1(1, 2, "s", 0, 64)
+        cast_w1(1, 2, "v", 64, 128)
+        quantize_w1(1, 2, 0, 2)
+        quantize_w1(1, 2, 2, 4)
+        planes["00"] = first_plane
+        planes["01"] = keep.tile([P, PACK, 512], BF16, name="planes_01")
+        drain_clip(planes["00"], 0, 0, range(4), 0, 512, wide)
         for a in range(KP):
             first_product(0, 1, a, 0, 256, a == 0, a == KP - 1)
         for t in range(PACK):
-            drain(4, 0, t, 0, 512, wide2[t])
-        for t in range(4):
-            clip(planes["01"], 0, t, wide2[t])
+            drain(0, 1, t, 0, 256, late[t])
         for t in range(PACK):
-            drain(0, 1, t, 0, 256, late[t][:, :256])
+            drain(4, 0, t, 0, 512, wide2[t])
         weave(planes["00"], 0, 256, woven[0], "s")
         for t in range(PACK):
-            clip(planes["10"], 1, t, late[t][:, :256])
+            clip(planes["10"], 1, t, late[t])
         weave(planes["10"], 0, 256, woven[1], "v")
         quantize_h(woven[1], 1, 0, 256)
-        for t in range(4, PACK):
-            clip(planes["01"], 0, t, wide2[t])
         quantize_h(woven[0], 0, 0, 256)
-        for a in (0, 2, 1):
-            first_product(4, 1, a, 256, 768, a == 0, a == 1)
-        spare = w1_raw[1, 1][:, 0, :].bitcast(BF16).rearrange("p (n t) -> p n t", t=PACK)
-        weave(planes["00"], 256, 512, spare, "s")
-        quantize_h(spare, 0, 256, 512)
-        drain_clip(planes["12"], 4, 1, range(2), 0, 512, wide)
-        forces(0, 0, 256, stage[2][:].rearrange("p t m j -> p (t m j)").bitcast(F32)[:, :256])
+        for t in range(4):
+            clip(planes["01"], 0, t, wide2[t])
+        for a in range(KP):
+            first_product(4, 1, a, 256, 768, a == 0, a == KP - 1)
+        both = stage[1][:].rearrange("p t m j -> p (t m j)")
+        drain_clip(planes["12"], 4, 1, range(4), 0, 512, wide)
+        forces(0, 0, 256)
         forces(1, 0, 256)
-        drain_clip(planes["12"], 4, 1, range(2, 4), 0, 512, wide)
-        forces(2, 0, 256)
-        weave(planes["01"], 0, 512, woven[2], "s")
-        quantize_h(woven[2], 0, 512, S)
-        weave(planes["12"], 0, 256, woven[0], "s")
-        quantize_h(woven[0], 1, 256, 512)
-        forces(3, 0, 256, wide[3][:, :256])
         for a in range(KP):
             first_product(4, 1, a, 768, S, a == 0, a == KP - 1)
-        drain_clip(planes["11"], 4, 1, range(4), 0, 256, half)
+        drain_clip(planes["11"], 4, 1, range(2), 0, 256, half)
+        weave(planes["12"], 0, 256, woven[1][:, 256:, :], "s")
+        quantize_h(woven[1][:, 256:, :], 1, 256, 512)
+        weave(planes["00"], 256, 512, woven[1], "s")
+        quantize_h(woven[1], 0, 256, 512)
+        forces(2, 0, 256, stage[0][:].rearrange("p t m j -> p (t m j)").bitcast(F32)[:, :256])
+        drain_clip(planes["11"], 4, 1, range(2, 4), 0, 256, half)
+        forces(3, 0, 256, both.bitcast(F32)[:, 384:640])
         forces(0, 256, 512)
-        weave(planes["12"], 256, 512, woven[1], "s")
-        quantize_h(woven[1], 1, 512, 768)
+        weave(planes["12"], 256, 512, woven[2], "s")
+        weave(planes["11"], 0, 256, woven[2][:, 256:, :], "s")
+        quantize_h(woven[2], 1, 512, S)
         forces(1, 256, 512)
-        weave(planes["11"], 0, 256, woven[0], "s")
-        quantize_h(woven[0], 1, 768, S)
-        forces(2, 256, 512, half[3])
-        forces(3, 256, 512)
+        weave(planes["01"], 0, 256, woven[0], "s")
+        weave(planes["01"], 256, 512, woven[0][:, 256:, :], "s")
+        quantize_h(woven[0], 0, 512, S)
+        forces(2, 256, 512, stage[2][:].rearrange("p t m j -> p (t m j)").bitcast(F32)[:, :256])
+        forces(3, 256, 512, stage[0][:].rearrange("p t m j -> p (t m j)").bitcast(F32)[:, :256])
         for nt in range(NT):
             forces(nt, 512, S)
             store(nt)

@@ -23,43 +23,51 @@ PASS = P * PACK
 KP = K // PASS
 HP = H // PASS
 NT = N // P
-WHOLE = ()
+LIST_ROWS = 16
+QUADRANTS = 4
+NARROW = 256
+FP4_N = 128
 HALVED = ((1, 0), (1, 2))
+SCALAR_SHARE_01 = 72
+SCALAR_SHARE_02 = 48
 
 
 def tile_list_yield_clipped_forces_kernel(tc, tab_words, tab_scales, w1, w2_words, w2_scales,
-                                                   s0, lo, hi, f0, wgo, offs, offs2, out):
+                                                      s0, lo, hi, f0, wgo, offs, offs2, out):
     nc = tc.nc
     with ExitStack() as ctx:
         keep = ctx.enter_context(tc.tile_pool(name="keep", bufs=1))
-        ring = ctx.enter_context(tc.tile_pool(name="ring", bufs=2))
         psum = ctx.enter_context(tc.psum_pool(name="psum", bufs=1))
 
-        gather_list = keep.tile([P, S // 16], U16, name="gather_list")
-        scatter_list = keep.tile([P, S // 16], U16, name="scatter_list")
+        gather_list = keep.tile([P, S // LIST_ROWS], U16, name="gather_list")
+        scatter_list = keep.tile([P, S // LIST_ROWS], U16, name="scatter_list")
         table = [keep.tile([P, T], I32, name="table%d" % a) for a in range(KP)]
         table_sc = keep.tile([P, T // 4], I32, name="table_sc")
         v_codes = [keep.tile([P, S], U32, name="v_codes%d" % a, align_bytes=64) for a in range(KP)]
         v_sc = keep.tile([P, S], U8, name="v_sc", align_bytes=64)
-        w1_rows = {a: keep.tile([P, PACK, H], F32, name="w1_rows%d" % a) for a in WHOLE}
-        w1_raw = {}
+
+        plane_words = PASS // 2
+        under_front = keep.tile([P, 2 * plane_words + PACK * PASS], F32, name="under_front", align_bytes=64)
+        under_back = keep.tile([P, plane_words + PACK * PASS // 2], F32, name="under_back", align_bytes=64)
+        planes0_front = under_front[:, :PACK * plane_words].bitcast(BF16).rearrange("p (t c) -> p t c", t=PACK)
+        planes0_back = under_back[:, :PACK * plane_words].bitcast(BF16).rearrange("p (t c) -> p t c", t=PACK)
+
+        w1_raw = {(1, 1): [under_front[:, 2 * plane_words:].rearrange("p (j c) -> p j c", j=PACK)],
+                  (1, 2): [under_back[:, plane_words:].rearrange("p (j c) -> p j c", j=PACK)]}
         w1_codes = {}
         w1_sc = {}
         for b in range(HP):
             for a in range(KP):
-                if a in WHOLE:
-                    w1_raw[b, a] = w1_rows[a][:, :, b * PASS:(b + 1) * PASS]
-                elif (b, a) in HALVED:
-                    w1_raw[b, a] = [keep.tile([P, PACK, PASS // 2], F32, name="w1_raw%d%d_%d" % (b, a, h), align_bytes=64)
-                                    for h in range(2)]
-                elif (b, a) != (1, 1):
-                    w1_raw[b, a] = keep.tile([P, PACK, PASS], F32, name="w1_raw%d%d" % (b, a), align_bytes=64)
+                parts = 2 if (b, a) in HALVED else 1
+                loaded = w1_raw.setdefault((b, a), [])
+                for part in range(len(loaded), parts):
+                    loaded.append(keep.tile([P, PACK, PASS // parts], F32, name="w1_raw%d%d_%d" % (b, a, part),
+                                            align_bytes=64)[:])
                 w1_codes[b, a] = keep.tile([P, PASS], U32, name="w1_codes%d%d" % (b, a), align_bytes=64)
                 w1_sc[b, a] = keep.tile([P, PASS], U8, name="w1_sc%d%d" % (b, a), align_bytes=64)
-        raw11 = keep.tile([P, 512 + PACK * PASS], F32, name="raw11", align_bytes=64)
-        w1_raw[1, 1] = raw11[:, 512:].rearrange("p (j c) -> p j c", j=PACK)
         w2_codes = keep.tile([P, HP, N // 2], I32, name="w2_codes", align_bytes=64)
         w2_sc = keep.tile([P, HP, N // 4], I32, name="w2_sc", align_bytes=64)
+        f0_row = 8
         vec_rows = keep.tile([P, PASS], F32, name="vec_rows")
         identity = keep.tile([P, P], F32, name="identity")
         row_consts = keep.tile([P, PACK, 3 * HP], F32, name="row_consts")
@@ -67,20 +75,29 @@ def tile_list_yield_clipped_forces_kernel(tc, tab_words, tab_scales, w1, w2_word
         wgo_sb = keep.tile([P, S], F32, name="wgo_sb")
         h_codes = [keep.tile([P, S], U32, name="h_codes%d" % b, align_bytes=64) for b in range(HP)]
         h_sc = [keep.tile([P, S], U8, name="h_sc%d" % b, align_bytes=64) for b in range(HP)]
+        second_codes = keep.tile([P, HP * NARROW], U32, name="second_codes", align_bytes=64)
+        second_sc = keep.tile([P, HP * NARROW], U8, name="second_sc", align_bytes=64)
         y_sb = [keep.tile([P, S], F32, name="y_sb%d" % nt) for nt in range(NT)]
         window = [keep.tile([P, T2], F32, name="window%d" % nt) for nt in range(NT)]
+        bank = [psum.tile([P, PASS], F32, name="bank%d" % i) for i in range(8)]
+        stage = [keep.tile([P, PACK, P, PACK], BF16, name="w1_stage%d" % a, align_bytes=64) for a in range(KP)]
+        woven = [stage[a][:].rearrange("p t m j -> p (t m) j") for a in range(KP)]
+        stage_flat = [stage[a][:].rearrange("p t m j -> p (t m j)") for a in range(KP)]
+        planes1_first = keep.tile([P, PACK, NARROW], BF16, name="planes1_first")
+        planes1_last = keep.tile([P, PACK, NARROW], BF16, name="planes1_last")
+        planes1_mid = keep.tile([P, PACK, PASS], BF16, name="planes1_mid")
+        trial = [keep.tile([P, PASS], F32, name="trial%d" % i) for i in range(8)]
+        trial_first = keep.tile([P, PACK * NARROW], F32, name="trial_first", align_bytes=64)
 
         def load_table(a):
             nc.sync.dma_start(table[a][:], tab_words[a].rearrange("p t i -> p (t i)").bitcast(I32))
 
-        def load_w1(b, a, c0, c1):
-            dst = w1_raw[b, a][2 * c0 // PASS][:] if (b, a) in HALVED else w1_raw[b, a][:, :, c0:c1]
-            nc.sync.dma_start(
-                dst,
-                w1[a * PASS:(a + 1) * PASS, b * PASS + c0:b * PASS + c1].rearrange("(p j) c -> p j c", j=PACK))
-
-        def load_rows(a):
-            nc.sync.dma_start(w1_rows[a][:], w1[a * PASS:(a + 1) * PASS, :].rearrange("(p j) c -> p j c", j=PACK))
+        def load_w1(b, a):
+            width = PASS // len(w1_raw[b, a])
+            for part, raw in enumerate(w1_raw[b, a]):
+                c0 = b * PASS + part * width
+                nc.sync.dma_start(
+                    raw, w1[a * PASS:(a + 1) * PASS, c0:c0 + width].rearrange("(p j) c -> p j c", j=PACK))
 
         nc.gpsimd.memset(table_sc[:], 0)
         nc.vector.memset(vec_rows[:], 0.0)
@@ -88,53 +105,42 @@ def tile_list_yield_clipped_forces_kernel(tc, tab_words, tab_scales, w1, w2_word
         make_identity(nc, identity[:])
         nc.sync.dma_start(gather_list[:], offs)
         load_table(0)
-        for q in range(4):
+        for q in range(QUADRANTS):
             nc.scalar.dma_start(table_sc[32 * q:32 * q + 4 * KP, :], tab_scales[:, 4 * q:4 * q + 4, :].bitcast(I32))
-        load_w1(0, 0, 0, PASS)
+        load_w1(0, 0)
         load_table(1)
         load_table(2)
         for i, vec in enumerate((s0, lo, hi)):
             nc.scalar.dma_start(vec_rows[HP * i:HP * (i + 1), :], vec.rearrange("(b c) -> b c", b=HP))
-        nc.scalar.dma_start(vec_rows[8:8 + NT, :P], f0.rearrange("(n p) -> n p", p=P))
-        load_w1(0, 1, 0, PASS)
-        load_w1(0, 2, 0, PASS)
-        load_w1(1, 0, 0, PASS // 2)
-        load_w1(1, 0, PASS // 2, PASS)
-        load_w1(1, 1, 0, PASS)
-        load_w1(1, 2, 0, PASS // 2)
-        load_w1(1, 2, PASS // 2, PASS)
+        nc.scalar.dma_start(vec_rows[f0_row:f0_row + NT, :P], f0.rearrange("(n p) -> n p", p=P))
+        load_w1(0, 1)
+        load_w1(0, 2)
+        for a in range(KP):
+            load_w1(1, a)
         nc.sync.dma_start(w2_codes[:], w2_words.rearrange("a p c -> p a c").bitcast(I32))
-        for q in range(4):
+        for q in range(QUADRANTS):
             nc.sync.dma_start(w2_sc[32 * q:32 * q + 4, :, :],
                               w2_scales[:, 4 * q:4 * q + 4, :].rearrange("a r n -> r a n").bitcast(I32))
         nc.sync.dma_start(scatter_list[:], offs2)
         nc.sync.dma_start(wgo_sb[:], wgo)
         for nt in range(NT):
-            (nc.vector if nt < 2 else nc.gpsimd).memset(window[nt][:], 0.0)
+            (nc.vector if nt < NT // 2 else nc.gpsimd).memset(window[nt][:], 0.0)
 
-        def gather_words(a, j0, j1):
-            nc.vector.tensor_copy(v_codes[a][:, j0:j1], table[a][:].bitcast(U32).indirect(gather_list[:, j0 // 16:j1 // 16]))
+        def gather_words(a):
+            nc.vector.tensor_copy(v_codes[a][:], table[a][:].bitcast(U32).indirect(gather_list[:]))
 
-        def gather_scales(j0, j1):
-            nc.vector.tensor_copy(v_sc[:, j0:j1], table_sc[:].bitcast(U8).indirect(gather_list[:, j0 // 16:j1 // 16]))
+        on_vector, on_scalar = nc.vector.tensor_copy, nc.scalar.copy
 
-        def copy_on(engine, dst, src):
-            if engine == "v":
-                nc.vector.tensor_copy(dst, src)
-            else:
-                nc.scalar.copy(dst, src)
-
-        def cast_w1(b, a, engine, m0, m1):
-            first = 64 * (m0 // 64) if (b, a) in HALVED else 0
-            raw = w1_raw[b, a][m0 // 64] if (b, a) in HALVED else w1_raw[b, a]
-            src = raw[:].rearrange("p j (m t) -> p m j t", t=PACK)
-            dst = w1_stage[b, a][:].rearrange("p t m j -> p m j t")
-            copy_on(engine, dst[:, m0:m1], src[:, m0 - first:m1 - first])
+        def round_w1(b, a, copier, m0, m1):
+            groups = P // len(w1_raw[b, a])
+            part = m0 // groups
+            src = w1_raw[b, a][part].rearrange("p j (m t) -> p m j t", t=PACK)
+            dst = stage[a][:].rearrange("p t m j -> p m j t")
+            copier(dst[:, m0:m1], src[:, m0 - part * groups:m1 - part * groups])
 
         def quantize_w1(b, a, t0, t1):
-            flat = w1_stage[b, a][:].rearrange("p t m j -> p (t m j)")
-            nc.vector.quantize_mx(out=w1_codes[b, a][:, t0 * P:t1 * P].bitcast(FP8X4), scales=w1_sc[b, a][:, t0 * P:t1 * P],
-                                  in_=flat[:, PASS * t0:PASS * t1])
+            nc.vector.quantize_mx(out=w1_codes[b, a][:, t0 * P:t1 * P].bitcast(FP8X4),
+                                  scales=w1_sc[b, a][:, t0 * P:t1 * P], in_=stage_flat[a][:, PASS * t0:PASS * t1])
 
         def first_product(first_bank, b, a, j0, j1, start, stop):
             for t in range(PACK):
@@ -146,140 +152,132 @@ def tile_list_yield_clipped_forces_kernel(tc, tab_words, tab_scales, w1, w2_word
                     rhs_scale=v_sc[4 * a:, j0:j1],
                     start=start, stop=stop)
 
-        def drain(first_bank, b, t, c0, c1, trial):
-            nc.scalar.activation(trial, bank[first_bank + t][:, c0:c1], IDENT, bias=row_consts[:, t, b:b + 1])
+        def all_passes(first_bank, b, j0, j1):
+            for a in range(KP):
+                first_product(first_bank, b, a, j0, j1, a == 0, a == KP - 1)
 
-        def clip(planes, b, t, trial):
-            nc.vector.tensor_scalar(planes[:, t, :], trial, row_consts[:, t, HP + b:HP + b + 1], row_consts[:, t, 2 * HP + b:2 * HP + b + 1], ALU.max, ALU.min)
+        def drain(first_bank, b, t, dst):
+            nc.scalar.activation(dst, bank[first_bank + t][:, :dst.shape[1]], IDENT, bias=row_consts[:, t, b:b + 1])
 
-        def drain_clip(planes, first_bank, b, ts, c0, c1, trials):
+        def clip(planes, b, t, src):
+            nc.vector.tensor_scalar(planes[:, t, :], src, row_consts[:, t, HP + b:HP + b + 1],
+                                    row_consts[:, t, 2 * HP + b:2 * HP + b + 1], ALU.max, ALU.min)
+
+        def drain_clip(planes, first_bank, b, ts, trials):
             for t in ts:
-                drain(first_bank, b, t, c0, c1, trials[t])
+                drain(first_bank, b, t, trials[t])
                 clip(planes, b, t, trials[t])
 
-        def weave(planes, c0, c1, grouped, engine):
-            copy_on(engine, grouped[:, :c1 - c0, :].rearrange("p (c i) t -> p c t i", i=4),
-                    planes[:, :, c0:c1].rearrange("p t (c i) -> p c t i", i=4))
+        def weave(copier, dst, planes, c0):
+            copier(dst.rearrange("p (c i) t -> p c t i", i=4),
+                   planes[:, :, c0:c0 + NARROW].rearrange("p t (c i) -> p c t i", i=4))
 
-        def quantize_h(grouped, b, j0, j1):
+        def quantize_h(src, b, j0, j1):
             nc.vector.quantize_mx(out=h_codes[b][:, j0:j1].bitcast(FP8X4), scales=h_sc[b][:, j0:j1],
-                                  in_=grouped[:, :j1 - j0, :].rearrange("p n t -> p (n t)"))
+                                  in_=src[:, :PACK * (j1 - j0)])
 
-        def second_product(acc, nt, j0, j1, y):
-            width = 512 if j1 - j0 == 512 else 128
+        def forces(nt, j0, j1, y):
+            width = PASS if j1 - j0 == PASS else FP4_N
             for b in range(HP):
+                codes, scales, shift = (second_codes, second_sc, NARROW * (b - 1)) if j0 == NARROW else (h_codes[b], h_sc[b], 0)
                 for g in range(j0, j1, width):
                     nc.tensor.matmul_mx(
-                        out=acc[:, g - j0:g - j0 + width],
+                        out=bank[nt][:, g - j0:g - j0 + width],
                         lhsT=w2_codes[:, b, :].bitcast(U8)[:, 2 * nt * P:2 * (nt + 1) * P].bitcast(FP4X4),
                         lhsT_scale=w2_sc[:, b, :].bitcast(U8)[:, nt * P:(nt + 1) * P],
-                        rhs=h_codes[b][:, g:g + width].bitcast(FP8X4),
-                        rhs_scale=h_sc[b][:, g:g + width],
+                        rhs=codes[:, g + shift:g + shift + width].bitcast(FP8X4),
+                        rhs_scale=scales[:, g + shift:g + shift + width],
                         start=(b == 0 and g == j0), stop=(b == HP - 1 and g == j1 - width))
-            nc.scalar.activation(y, acc[:, :j1 - j0], IDENT, bias=f0_sb[:, nt:nt + 1])
+            nc.scalar.activation(y, bank[nt][:, :j1 - j0], IDENT, bias=f0_sb[:, nt:nt + 1])
+            nc.vector.tensor_tensor(window[nt][:].indirect(scatter_list[:, j0 // LIST_ROWS:j1 // LIST_ROWS]),
+                                    y, wgo_sb[:, j0:j1], ALU.mult)
 
-        def scatter(nt, j0, j1, y):
-            nc.vector.tensor_tensor(window[nt][:].indirect(scatter_list[:, j0 // 16:j1 // 16]), y, wgo_sb[:, j0:j1], ALU.mult)
+        def y_on_stage(a, word0):
+            return stage_flat[a].bitcast(F32)[:, word0:word0 + NARROW]
 
-        def store(nt):
-            nc.sync.dma_start(out[nt * P:(nt + 1) * P, :], window[nt][:])
-
-        bank = [psum.tile([P, PASS], F32, name="bank%d" % i) for i in range(8)]
-        stage = [keep.tile([P, PACK, P, PACK], BF16, name="w1_stage%d" % i, align_bytes=64) for i in range(3)]
-        w1_stage = {(b, a): stage[a] for b in range(HP) for a in range(KP)}
-
-        woven = [stage[i][:].rearrange("p t m j -> p (t m) j") for i in range(3)]
-        planes = {key: keep.tile([P, PACK, width], BF16, name="planes_" + key)
-                  for key, width in (("10", 256), ("11", 256), ("12", 512))}
-        trial = [keep.tile([P, PASS], F32, name="trial%d" % i) for i in range(8)]
-        late_all = keep.tile([P, PACK * 256], F32, name="late", align_bytes=64)
-        late = [late_all[:, 256 * t:256 * (t + 1)] for t in range(PACK)]
-        first_plane = raw11[:, :1024].bitcast(BF16).rearrange("p (t c) -> p t c", t=PACK)
-        wide = [trial[t][:] for t in range(4)]
-        wide2 = [trial[4 + t][:] for t in range(4)]
-        half = [trial[4 + t][:, :256] for t in range(4)]
-
-        def forces(nt, j0, j1, y=None):
-            y = y_sb[nt][:, j0:j1] if y is None else y
-            second_product(bank[nt], nt, j0, j1, y)
-            scatter(nt, j0, j1, y)
+        front = [trial[t][:] for t in range(PACK)]
+        back = [trial[PACK + t][:] for t in range(PACK)]
+        back_narrow = [trial[PACK + t][:, :NARROW] for t in range(PACK)]
+        first = [trial_first[:, NARROW * t:NARROW * (t + 1)] for t in range(PACK)]
+        lower = [woven[a][:, :NARROW, :] for a in range(KP)]
+        upper = [woven[a][:, NARROW:, :] for a in range(KP)]
+        r0, r1, r2, r3 = 0, NARROW, 2 * NARROW, 3 * NARROW
 
         for t in range(PACK):
             nc.tensor.transpose(bank[0][:, t * P:(t + 1) * P], vec_rows[:, t:PASS:PACK], identity[:])
         nc.tensor.transpose(bank[1][:, :P], vec_rows[:, :P], identity[:])
         nc.scalar.copy(row_consts[:], bank[0][:].rearrange("p (t r) -> p t r", t=PACK)[:, :, :3 * HP])
-        nc.scalar.copy(f0_sb[:], bank[1][:, 8:8 + NT])
-        gather_words(0, 0, S)
-        gather_scales(0, S)
-        gather_words(1, 0, S)
-        cast_w1(0, 0, "s", 0, 128)
-        quantize_w1(0, 0, 0, 4)
-        gather_words(2, 0, S)
-        first_product(0, 0, 0, 0, 512, True, False)
-        first_product(4, 0, 0, 512, S, True, False)
-        cast_w1(0, 1, "s", 0, 72)
-        cast_w1(0, 1, "v", 72, 128)
-        quantize_w1(0, 1, 0, 4)
-        first_product(0, 0, 1, 0, 512, False, False)
-        cast_w1(0, 2, "s", 0, 48)
-        cast_w1(0, 2, "v", 48, 128)
+        nc.scalar.copy(f0_sb[:], bank[1][:, f0_row:f0_row + NT])
+
+        gather_words(0)
+        nc.vector.tensor_copy(v_sc[:], table_sc[:].bitcast(U8).indirect(gather_list[:]))
+        gather_words(1)
+        round_w1(0, 0, on_scalar, 0, P)
+        quantize_w1(0, 0, 0, PACK)
+        gather_words(2)
+        first_product(0, 0, 0, r0, r2, True, False)
+        first_product(4, 0, 0, r2, S, True, False)
+        round_w1(0, 1, on_scalar, 0, SCALAR_SHARE_01)
+        round_w1(0, 1, on_vector, SCALAR_SHARE_01, P)
+        quantize_w1(0, 1, 0, PACK)
+        first_product(0, 0, 1, r0, r2, False, False)
+        round_w1(0, 2, on_scalar, 0, SCALAR_SHARE_02)
+        round_w1(0, 2, on_vector, SCALAR_SHARE_02, P)
         quantize_w1(0, 2, 0, 2)
-        quantize_w1(0, 2, 2, 4)
-        first_product(0, 0, 2, 0, 512, False, True)
-        first_product(4, 0, 2, 512, S, False, False)
-        first_product(4, 0, 1, 512, S, False, True)
-        cast_w1(1, 0, "s", 0, 64)
-        cast_w1(1, 0, "v", 64, 128)
-        quantize_w1(1, 0, 0, 4)
-        cast_w1(1, 1, "v", 0, 128)
-        quantize_w1(1, 1, 0, 4)
-        cast_w1(1, 2, "s", 0, 64)
-        cast_w1(1, 2, "v", 64, 128)
+        quantize_w1(0, 2, 2, PACK)
+        first_product(0, 0, 2, r0, r2, False, True)
+        first_product(4, 0, 2, r2, S, False, False)
+        first_product(4, 0, 1, r2, S, False, True)
+
+        round_w1(1, 0, on_scalar, 0, P // 2)
+        round_w1(1, 0, on_vector, P // 2, P)
+        quantize_w1(1, 0, 0, PACK)
+        round_w1(1, 1, on_vector, 0, P)
+        quantize_w1(1, 1, 0, PACK)
+        round_w1(1, 2, on_scalar, 0, P // 2)
+        round_w1(1, 2, on_vector, P // 2, P)
         quantize_w1(1, 2, 0, 2)
-        quantize_w1(1, 2, 2, 4)
-        planes["00"] = first_plane
-        planes["01"] = keep.tile([P, PACK, 512], BF16, name="planes_01")
-        drain_clip(planes["00"], 0, 0, range(4), 0, 512, wide)
-        for a in range(KP):
-            first_product(0, 1, a, 0, 256, a == 0, a == KP - 1)
+        quantize_w1(1, 2, 2, PACK)
+        drain_clip(planes0_front, 0, 0, range(PACK), front)
+
+        all_passes(0, 1, r0, r1)
         for t in range(PACK):
-            drain(0, 1, t, 0, 256, late[t])
+            drain(0, 1, t, first[t])
         for t in range(PACK):
-            drain(4, 0, t, 0, 512, wide2[t])
-        weave(planes["00"], 0, 256, woven[0], "s")
+            drain(4, 0, t, back[t])
+        weave(on_scalar, lower[0], planes0_front, 0)
         for t in range(PACK):
-            clip(planes["10"], 1, t, late[t])
-        weave(planes["10"], 0, 256, woven[1], "v")
-        quantize_h(woven[1], 1, 0, 256)
-        quantize_h(woven[0], 0, 0, 256)
-        for t in range(4):
-            clip(planes["01"], 0, t, wide2[t])
-        for a in range(KP):
-            first_product(4, 1, a, 256, 768, a == 0, a == KP - 1)
-        both = stage[1][:].rearrange("p t m j -> p (t m j)")
-        drain_clip(planes["12"], 4, 1, range(4), 0, 512, wide)
-        forces(0, 0, 256)
-        forces(1, 0, 256)
-        for a in range(KP):
-            first_product(4, 1, a, 768, S, a == 0, a == KP - 1)
-        drain_clip(planes["11"], 4, 1, range(2), 0, 256, half)
-        weave(planes["12"], 0, 256, woven[1][:, 256:, :], "s")
-        quantize_h(woven[1][:, 256:, :], 1, 256, 512)
-        weave(planes["00"], 256, 512, woven[1], "s")
-        quantize_h(woven[1], 0, 256, 512)
-        forces(2, 0, 256, stage[0][:].rearrange("p t m j -> p (t m j)").bitcast(F32)[:, :256])
-        drain_clip(planes["11"], 4, 1, range(2, 4), 0, 256, half)
-        forces(3, 0, 256, both.bitcast(F32)[:, 384:640])
-        forces(0, 256, 512)
-        weave(planes["12"], 256, 512, woven[2], "s")
-        weave(planes["11"], 0, 256, woven[2][:, 256:, :], "s")
-        quantize_h(woven[2], 1, 512, S)
-        forces(1, 256, 512)
-        weave(planes["01"], 0, 256, woven[0], "s")
-        weave(planes["01"], 256, 512, woven[0][:, 256:, :], "s")
-        quantize_h(woven[0], 0, 512, S)
-        forces(2, 256, 512, stage[2][:].rearrange("p t m j -> p (t m j)").bitcast(F32)[:, :256])
-        forces(3, 256, 512, stage[0][:].rearrange("p t m j -> p (t m j)").bitcast(F32)[:, :256])
+            clip(planes1_first, 1, t, first[t])
+        weave(on_vector, lower[1], planes1_first, 0)
+        quantize_h(stage_flat[1], 1, r0, r1)
+        quantize_h(stage_flat[0], 0, r0, r1)
+        for t in range(PACK):
+            clip(planes0_back, 0, t, back[t])
+        all_passes(4, 1, r1, r3)
+        drain_clip(planes1_mid, 4, 1, range(PACK), front)
+        forces(0, r0, r1, y_sb[0][:, r0:r1])
+        forces(1, r0, r1, y_sb[1][:, r0:r1])
+
+        all_passes(4, 1, r3, S)
+        drain_clip(planes1_last, 4, 1, range(2), back_narrow)
+        weave(on_scalar, upper[1], planes1_mid, 0)
+        weave(on_scalar, lower[1], planes0_front, NARROW)
+        nc.vector.quantize_mx(out=second_codes[:].bitcast(FP8X4), scales=second_sc[:], in_=stage_flat[1])
+        forces(2, r0, r1, y_on_stage(0, 0))
+        drain_clip(planes1_last, 4, 1, range(2, PACK), back_narrow)
+        forces(3, r0, r1, y_on_stage(1, 3 * NARROW // 2))
+
+        forces(0, r1, r2, y_sb[0][:, r1:r2])
+        weave(on_scalar, lower[2], planes1_mid, NARROW)
+        weave(on_scalar, upper[2], planes1_last, 0)
+        quantize_h(stage_flat[2], 1, r2, S)
+        forces(1, r1, r2, y_sb[1][:, r1:r2])
+        weave(on_scalar, lower[0], planes0_back, 0)
+        weave(on_scalar, upper[0], planes0_back, NARROW)
+        quantize_h(stage_flat[0], 0, r2, S)
+        forces(2, r1, r2, y_on_stage(2, 0))
+        forces(3, r1, r2, y_on_stage(0, 0))
+
         for nt in range(NT):
-            forces(nt, 512, S)
-            store(nt)
+            forces(nt, r2, S, y_sb[nt][:, r2:])
+            nc.sync.dma_start(out[nt * P:(nt + 1) * P, :], window[nt][:])

@@ -105,14 +105,14 @@ def tile_list_yield_clipped_forces_kernel(tc, tab_words, tab_scales, w1, w2_word
         make_identity(nc, identity[:])
         nc.sync.dma_start(gather_list[:], offs)
         load_table(0)
-        for q in range(QUADRANTS):
-            nc.scalar.dma_start(table_sc[32 * q:32 * q + 4 * KP, :], tab_scales[:, 4 * q:4 * q + 4, :].bitcast(I32))
-        load_w1(0, 0)
         load_table(1)
-        load_table(2)
+        for q in range(QUADRANTS):
+            nc.sync.dma_start(table_sc[32 * q:32 * q + 4 * KP, :], tab_scales[:, 4 * q:4 * q + 4, :].bitcast(I32))
+        load_w1(0, 0)
         for i, vec in enumerate((s0, lo, hi)):
-            nc.scalar.dma_start(vec_rows[HP * i:HP * (i + 1), :], vec.rearrange("(b c) -> b c", b=HP))
-        nc.scalar.dma_start(vec_rows[f0_row:f0_row + NT, :P], f0.rearrange("(n p) -> n p", p=P))
+            nc.sync.dma_start(vec_rows[HP * i:HP * (i + 1), :], vec.rearrange("(b c) -> b c", b=HP))
+        nc.sync.dma_start(vec_rows[f0_row:f0_row + NT, :P], f0.rearrange("(n p) -> n p", p=P))
+        load_table(2)
         load_w1(0, 1)
         load_w1(0, 2)
         for a in range(KP):

@@ -29,7 +29,8 @@ NARROW = 256
 FP4_N = 128
 HALVED = ((1, 0), (1, 2))
 SCALAR_SHARE_01 = 72
-SCALAR_SHARE_02 = 48
+SCALAR_SHARE_02 = 36
+SCALAR_SHARE_10 = 44
 
 
 def tile_list_yield_clipped_forces_kernel(tc, tab_words, tab_scales, w1, w2_words, w2_scales,
@@ -47,13 +48,17 @@ def tile_list_yield_clipped_forces_kernel(tc, tab_words, tab_scales, w1, w2_word
         v_sc = keep.tile([P, S], U8, name="v_sc", align_bytes=64)
 
         plane_words = PASS // 2
-        under_front = keep.tile([P, 2 * plane_words + PACK * PASS], F32, name="under_front", align_bytes=64)
-        under_back = keep.tile([P, plane_words + PACK * PASS // 2], F32, name="under_back", align_bytes=64)
-        planes0_front = under_front[:, :PACK * plane_words].bitcast(BF16).rearrange("p (t c) -> p t c", t=PACK)
-        planes0_back = under_back[:, :PACK * plane_words].bitcast(BF16).rearrange("p (t c) -> p t c", t=PACK)
+        piece_words = PACK * PASS
+        planes0_front = keep.tile([P, PACK, PASS], BF16, name="planes0_front")
+        under_back = keep.tile([P, piece_words + piece_words // 2], F32, name="under_back", align_bytes=64)
+        under_first = keep.tile([P, piece_words // 2], F32, name="under_first", align_bytes=64)
+        planes0_back = under_back[:, piece_words - 2 * plane_words:piece_words + 2 * plane_words].bitcast(BF16).rearrange(
+            "p (t c) -> p t c", t=PACK)
+        woven0_first = under_first[:, :PACK * NARROW // 2].bitcast(BF16)
 
-        w1_raw = {(1, 1): [under_front[:, 2 * plane_words:].rearrange("p (j c) -> p j c", j=PACK)],
-                  (1, 2): [under_back[:, plane_words:].rearrange("p (j c) -> p j c", j=PACK)]}
+        w1_raw = {(1, 1): [under_back[:, :piece_words].rearrange("p (j c) -> p j c", j=PACK)],
+                  (1, 2): [under_first[:].rearrange("p (j c) -> p j c", j=PACK),
+                           under_back[:, piece_words:].rearrange("p (j c) -> p j c", j=PACK)]}
         w1_codes = {}
         w1_sc = {}
         for b in range(HP):
@@ -131,16 +136,22 @@ def tile_list_yield_clipped_forces_kernel(tc, tab_words, tab_scales, w1, w2_word
 
         on_vector, on_scalar = nc.vector.tensor_copy, nc.scalar.copy
 
-        def round_w1(b, a, copier, m0, m1):
+        def round_w1(b, a, copier, m0, m1, t0=0, t1=PACK):
             groups = P // len(w1_raw[b, a])
             part = m0 // groups
             src = w1_raw[b, a][part].rearrange("p j (m t) -> p m j t", t=PACK)
             dst = stage[a][:].rearrange("p t m j -> p m j t")
-            copier(dst[:, m0:m1], src[:, m0 - part * groups:m1 - part * groups])
+            copier(dst[:, m0:m1, :, t0:t1], src[:, m0 - part * groups:m1 - part * groups, :, t0:t1])
 
         def quantize_w1(b, a, t0, t1):
             nc.vector.quantize_mx(out=w1_codes[b, a][:, t0 * P:t1 * P].bitcast(FP8X4),
                                   scales=w1_sc[b, a][:, t0 * P:t1 * P], in_=stage_flat[a][:, PASS * t0:PASS * t1])
+
+        def round_in_pairs(b, a, m0):
+            for t0 in (0, 2):
+                round_w1(b, a, on_vector, m0, P, t0, t0 + 2)
+            for t0 in (0, 2):
+                quantize_w1(b, a, t0, t0 + 2)
 
         def first_product(first_bank, b, a, j0, j1, start, stop):
             for t in range(PACK):
@@ -222,35 +233,33 @@ def tile_list_yield_clipped_forces_kernel(tc, tab_words, tab_scales, w1, w2_word
         quantize_w1(0, 1, 0, PACK)
         first_product(0, 0, 1, r0, r2, False, False)
         round_w1(0, 2, on_scalar, 0, SCALAR_SHARE_02)
-        round_w1(0, 2, on_vector, SCALAR_SHARE_02, P)
-        quantize_w1(0, 2, 0, 2)
-        quantize_w1(0, 2, 2, PACK)
+        round_in_pairs(0, 2, SCALAR_SHARE_02)
         first_product(0, 0, 2, r0, r2, False, True)
         first_product(4, 0, 2, r2, S, False, False)
         first_product(4, 0, 1, r2, S, False, True)
 
-        round_w1(1, 0, on_scalar, 0, P // 2)
+        round_w1(1, 0, on_scalar, 0, SCALAR_SHARE_10)
+        round_w1(1, 0, on_vector, SCALAR_SHARE_10, P // 2)
         round_w1(1, 0, on_vector, P // 2, P)
         quantize_w1(1, 0, 0, PACK)
-        round_w1(1, 1, on_vector, 0, P)
-        quantize_w1(1, 1, 0, PACK)
+        round_in_pairs(1, 1, 0)
         round_w1(1, 2, on_scalar, 0, P // 2)
-        round_w1(1, 2, on_vector, P // 2, P)
-        quantize_w1(1, 2, 0, 2)
-        quantize_w1(1, 2, 2, PACK)
+        round_in_pairs(1, 2, P // 2)
         drain_clip(planes0_front, 0, 0, range(PACK), front)
 
         all_passes(0, 1, r0, r1)
-        for t in range(PACK):
+        last_t = PACK - 1
+        nc.vector.tensor_scalar(first[last_t], bank[last_t][:, :NARROW], row_consts[:, last_t, 1:2], None, ALU.add)
+        for t in range(last_t):
             drain(0, 1, t, first[t])
         for t in range(PACK):
             drain(4, 0, t, back[t])
-        weave(on_scalar, lower[0], planes0_front, 0)
-        for t in range(PACK):
+        weave(on_scalar, woven0_first.rearrange("p (c t) -> p c t", t=PACK), planes0_front, 0)
+        for t in (0, last_t, 1, 2):
             clip(planes1_first, 1, t, first[t])
         weave(on_vector, lower[1], planes1_first, 0)
         quantize_h(stage_flat[1], 1, r0, r1)
-        quantize_h(stage_flat[0], 0, r0, r1)
+        quantize_h(woven0_first, 0, r0, r1)
         for t in range(PACK):
             clip(planes0_back, 0, t, back[t])
         all_passes(4, 1, r1, r3)
@@ -263,7 +272,7 @@ def tile_list_yield_clipped_forces_kernel(tc, tab_words, tab_scales, w1, w2_word
         weave(on_scalar, upper[1], planes1_mid, 0)
         weave(on_scalar, lower[1], planes0_front, NARROW)
         nc.vector.quantize_mx(out=second_codes[:].bitcast(FP8X4), scales=second_sc[:], in_=stage_flat[1])
-        forces(2, r0, r1, y_on_stage(0, 0))
+        forces(2, r0, r1, y_on_stage(0, 3 * NARROW // 2))
         drain_clip(planes1_last, 4, 1, range(2, PACK), back_narrow)
         forces(3, r0, r1, y_on_stage(1, 3 * NARROW // 2))
 

@@ -72,10 +72,10 @@ def tile_list_yield_clipped_forces_kernel(tc, tab_words, tab_scales, w1, w2_word
                 w1_sc[b, a] = keep.tile([P, PASS], U8, name="w1_sc%d%d" % (b, a), align_bytes=64)
         w2_codes = keep.tile([P, HP, N // 2], I32, name="w2_codes", align_bytes=64)
         w2_sc = keep.tile([P, HP, N // 4], I32, name="w2_sc", align_bytes=64)
-        f0_row = 8
+        f0_rows = slice(12, P, 32)
         vec_rows = keep.tile([P, PASS], F32, name="vec_rows")
         identity = keep.tile([P, P], F32, name="identity")
-        row_consts = keep.tile([P, PACK, 3 * HP], F32, name="row_consts")
+        row_consts = keep.tile([P, PACK, HP, 3], F32, name="row_consts")
         f0_sb = keep.tile([P, NT], F32, name="f0_sb")
         wgo_sb = keep.tile([P, S], F32, name="wgo_sb")
         h_codes = [keep.tile([P, S], U32, name="h_codes%d" % b, align_bytes=64) for b in range(HP)]
@@ -111,12 +111,12 @@ def tile_list_yield_clipped_forces_kernel(tc, tab_words, tab_scales, w1, w2_word
         nc.sync.dma_start(gather_list[:], offs)
         load_table(0)
         load_table(1)
-        for q in range(QUADRANTS):
+        for q in (0, 2, 1, 3):
             nc.sync.dma_start(table_sc[32 * q:32 * q + 4 * KP, :], tab_scales[:, 4 * q:4 * q + 4, :].bitcast(I32))
         load_w1(0, 0)
         for i, vec in enumerate((s0, lo, hi)):
-            nc.sync.dma_start(vec_rows[HP * i:HP * (i + 1), :], vec.rearrange("(b c) -> b c", b=HP))
-        nc.sync.dma_start(vec_rows[f0_row:f0_row + NT, :P], f0.rearrange("(n p) -> n p", p=P))
+            nc.sync.dma_start(vec_rows[4 * i:P:64, :], vec.rearrange("(b c) -> b c", b=HP))
+        nc.sync.dma_start(vec_rows[f0_rows, :P], f0.rearrange("(n p) -> n p", p=P))
         load_table(2)
         load_w1(0, 1)
         load_w1(0, 2)
@@ -168,11 +168,10 @@ def tile_list_yield_clipped_forces_kernel(tc, tab_words, tab_scales, w1, w2_word
                 first_product(first_bank, b, a, j0, j1, a == 0, a == KP - 1)
 
         def drain(first_bank, b, t, dst):
-            nc.scalar.activation(dst, bank[first_bank + t][:, :dst.shape[1]], IDENT, bias=row_consts[:, t, b:b + 1])
+            nc.scalar.activation(dst, bank[first_bank + t][:, :dst.shape[1]], IDENT, bias=row_consts[:, t, b, 0:1])
 
         def clip(planes, b, t, src):
-            nc.vector.tensor_scalar(planes[:, t, :], src, row_consts[:, t, HP + b:HP + b + 1],
-                                    row_consts[:, t, 2 * HP + b:2 * HP + b + 1], ALU.max, ALU.min)
+            nc.vector.tensor_scalar(planes[:, t, :], src, row_consts[:, t, b, 1:2], row_consts[:, t, b, 2:3], ALU.max, ALU.min)
 
         def drain_clip(planes, first_bank, b, ts, trials):
             for t in ts:
@@ -217,8 +216,8 @@ def tile_list_yield_clipped_forces_kernel(tc, tab_words, tab_scales, w1, w2_word
         for t in range(PACK):
             nc.tensor.transpose(bank[0][:, t * P:(t + 1) * P], vec_rows[:, t:PASS:PACK], identity[:])
         nc.tensor.transpose(bank[1][:, :P], vec_rows[:, :P], identity[:])
-        nc.scalar.copy(row_consts[:], bank[0][:].rearrange("p (t r) -> p t r", t=PACK)[:, :, :3 * HP])
-        nc.scalar.copy(f0_sb[:], bank[1][:, f0_row:f0_row + NT])
+        nc.scalar.copy(row_consts[:], bank[0][:].rearrange("p (t b r) -> p t b r", t=PACK, b=HP)[:, :, :, 0:12:4])
+        nc.scalar.copy(f0_sb[:], bank[1][:, f0_rows])
 
         gather_words(0)
         nc.vector.tensor_copy(v_sc[:], table_sc[:].bitcast(U8).indirect(gather_list[:]))
@@ -249,7 +248,7 @@ def tile_list_yield_clipped_forces_kernel(tc, tab_words, tab_scales, w1, w2_word
 
         all_passes(0, 1, r0, r1)
         last_t = PACK - 1
-        nc.vector.tensor_scalar(first[last_t], bank[last_t][:, :NARROW], row_consts[:, last_t, 1:2], None, ALU.add)
+        nc.vector.tensor_scalar(first[last_t], bank[last_t][:, :NARROW], row_consts[:, last_t, 1, 0:1], None, ALU.add)
         for t in range(last_t):
             drain(0, 1, t, first[t])
         for t in range(PACK):

@@ -42,10 +42,9 @@ def tile_list_yield_clipped_forces_kernel(tc, tab_words, tab_scales, w1, w2_word
 
         gather_list = keep.tile([P, S // LIST_ROWS], U16, name="gather_list")
         scatter_list = keep.tile([P, S // LIST_ROWS], U16, name="scatter_list")
-        table = [keep.tile([P, T], I32, name="table%d" % a) for a in range(KP)]
+        table = [keep.tile([P, T], I32, name="table%d" % a, tag="table%d" % a, align_bytes=64) for a in range(KP)]
         table_sc = keep.tile([P, T // 4], I32, name="table_sc")
         v_codes = [keep.tile([P, S], U32, name="v_codes%d" % a, align_bytes=64) for a in range(KP)]
-        v_sc = keep.tile([P, S], U8, name="v_sc", align_bytes=64)
 
         plane_words = PASS // 2
         piece_words = PACK * PASS
@@ -73,7 +72,7 @@ def tile_list_yield_clipped_forces_kernel(tc, tab_words, tab_scales, w1, w2_word
         w2_codes = keep.tile([P, HP, N // 2], I32, name="w2_codes", align_bytes=64)
         w2_sc = keep.tile([P, HP, N // 4], I32, name="w2_sc", align_bytes=64)
         f0_rows = slice(12, P, 32)
-        vec_rows = keep.tile([P, PASS], F32, name="vec_rows")
+        vec_rows = keep.tile([P, PASS], F32, name="vec_rows", tag="vec_rows", align_bytes=64)
         identity = keep.tile([P, P], F32, name="identity")
         row_consts = keep.tile([P, PACK, HP, 3], F32, name="row_consts")
         f0_sb = keep.tile([P, NT], F32, name="f0_sb")
@@ -83,9 +82,10 @@ def tile_list_yield_clipped_forces_kernel(tc, tab_words, tab_scales, w1, w2_word
         second_codes = keep.tile([P, HP * NARROW], U32, name="second_codes", align_bytes=64)
         second_sc = keep.tile([P, HP * NARROW], U8, name="second_sc", align_bytes=64)
         y_sb = [keep.tile([P, S], F32, name="y_sb%d" % nt) for nt in range(NT)]
-        window = [keep.tile([P, T2], F32, name="window%d" % nt) for nt in range(NT)]
+        window = [keep.tile([P, T2], F32, name="window0")]
         bank = [psum.tile([P, PASS], F32, name="bank%d" % i) for i in range(8)]
         stage = [keep.tile([P, PACK, P, PACK], BF16, name="w1_stage%d" % a, align_bytes=64) for a in range(KP)]
+        first_stage = keep.tile([P, PACK, P, PACK], BF16, name="first_stage", tag="first_stage", align_bytes=64)
         woven = [stage[a][:].rearrange("p t m j -> p (t m) j") for a in range(KP)]
         stage_flat = [stage[a][:].rearrange("p t m j -> p (t m j)") for a in range(KP)]
         planes1_first = keep.tile([P, PACK, NARROW], BF16, name="planes1_first")
@@ -104,48 +104,59 @@ def tile_list_yield_clipped_forces_kernel(tc, tab_words, tab_scales, w1, w2_word
                 nc.sync.dma_start(
                     raw, w1[a * PASS:(a + 1) * PASS, c0:c0 + width].rearrange("(p j) c -> p j c", j=PACK))
 
+        def load_w2_scales(q):
+            nc.sync.dma_start(w2_sc[32 * q:32 * q + 4, :, :],
+                              w2_scales[:, 4 * q:4 * q + 4, :].rearrange("a r n -> r a n").bitcast(I32))
+
         nc.gpsimd.memset(table_sc[:], 0)
         nc.vector.memset(vec_rows[:], 0.0)
-        nc.gpsimd.memset(w2_sc[:], 0)
+        nc.vector.memset(w2_sc[:], 0)
         make_identity(nc, identity[:])
         nc.sync.dma_start(gather_list[:], offs)
         load_table(0)
         load_table(1)
         for q in (0, 2, 1, 3):
-            nc.sync.dma_start(table_sc[32 * q:32 * q + 4 * KP, :], tab_scales[:, 4 * q:4 * q + 4, :].bitcast(I32))
-        load_w1(0, 0)
+            nc.gpsimd.dma_start(table_sc[32 * q:32 * q + 4 * KP, :], tab_scales[:, 4 * q:4 * q + 4, :].bitcast(I32))
         for i, vec in enumerate((s0, lo, hi)):
             nc.sync.dma_start(vec_rows[4 * i:P:64, :], vec.rearrange("(b c) -> b c", b=HP))
         nc.sync.dma_start(vec_rows[f0_rows, :P], f0.rearrange("(n p) -> n p", p=P))
+        load_w2_scales(0)
+        load_w2_scales(1)
+        load_w1(0, 0)
         load_table(2)
         load_w1(0, 1)
         load_w1(0, 2)
         for a in range(KP):
             load_w1(1, a)
         nc.sync.dma_start(w2_codes[:], w2_words.rearrange("a p c -> p a c").bitcast(I32))
-        for q in range(QUADRANTS):
-            nc.sync.dma_start(w2_sc[32 * q:32 * q + 4, :, :],
-                              w2_scales[:, 4 * q:4 * q + 4, :].rearrange("a r n -> r a n").bitcast(I32))
+        for q in range(2, QUADRANTS):
+            load_w2_scales(q)
         nc.sync.dma_start(scatter_list[:], offs2)
         nc.sync.dma_start(wgo_sb[:], wgo)
-        for nt in range(NT):
-            (nc.vector if nt < NT // 2 else nc.gpsimd).memset(window[nt][:], 0.0)
+        nc.vector.memset(window[0][:], 0.0)
+
+        def zero_window(under):
+            window.append(keep.tile([P, T2], F32, name="window%d" % len(window), tag=under, align_bytes=64))
+            nc.gpsimd.memset(window[-1][:], 0.0)
 
         def gather_words(a):
             nc.vector.tensor_copy(v_codes[a][:], table[a][:].bitcast(U32).indirect(gather_list[:]))
 
         on_vector, on_scalar = nc.vector.tensor_copy, nc.scalar.copy
 
+        def rounded(b, a):
+            return first_stage[:] if (b, a) == (0, 0) else stage[a][:]
+
         def round_w1(b, a, copier, m0, m1, t0=0, t1=PACK):
             groups = P // len(w1_raw[b, a])
             part = m0 // groups
             src = w1_raw[b, a][part].rearrange("p j (m t) -> p m j t", t=PACK)
-            dst = stage[a][:].rearrange("p t m j -> p m j t")
+            dst = rounded(b, a).rearrange("p t m j -> p m j t")
             copier(dst[:, m0:m1, :, t0:t1], src[:, m0 - part * groups:m1 - part * groups, :, t0:t1])
 
         def quantize_w1(b, a, t0, t1):
             nc.vector.quantize_mx(out=w1_codes[b, a][:, t0 * P:t1 * P].bitcast(FP8X4),
-                                  scales=w1_sc[b, a][:, t0 * P:t1 * P], in_=stage_flat[a][:, PASS * t0:PASS * t1])
+                                  scales=w1_sc[b, a][:, t0 * P:t1 * P], in_=rounded(b, a).rearrange("p t m j -> p (t m j)")[:, PASS * t0:PASS * t1])
 
         def round_in_pairs(b, a, m0):
             for t0 in (0, 2):
@@ -220,10 +231,14 @@ def tile_list_yield_clipped_forces_kernel(tc, tab_words, tab_scales, w1, w2_word
         nc.scalar.copy(f0_sb[:], bank[1][:, f0_rows])
 
         gather_words(0)
-        nc.vector.tensor_copy(v_sc[:], table_sc[:].bitcast(U8).indirect(gather_list[:]))
+        zero_window("table0")
+        zero_window("vec_rows")
         gather_words(1)
+        v_sc = keep.tile([P, S], U8, name="v_sc", tag="table1", align_bytes=64)
+        nc.vector.tensor_copy(v_sc[:], table_sc[:].bitcast(U8).indirect(gather_list[:]))
         round_w1(0, 0, on_scalar, 0, P)
         quantize_w1(0, 0, 0, PACK)
+        zero_window("first_stage")
         gather_words(2)
         first_product(0, 0, 0, r0, r2, True, False)
         first_product(4, 0, 0, r2, S, True, False)

@@ -89,10 +89,14 @@ def tile_list_yield_clipped_forces_kernel(tc, tab_words, tab_scales, w1, w2_word
         woven = [stage[a][:].rearrange("p t m j -> p (t m) j") for a in range(KP)]
         stage_flat = [stage[a][:].rearrange("p t m j -> p (t m j)") for a in range(KP)]
         planes1_first = keep.tile([P, PACK, NARROW], BF16, name="planes1_first")
-        planes1_last = keep.tile([P, PACK, NARROW], BF16, name="planes1_last")
-        planes1_mid = keep.tile([P, PACK, PASS], BF16, name="planes1_mid")
+        first_weighted = keep.tile([P, NARROW], F32, name="first_weighted")
         trial = [keep.tile([P, PASS], F32, name="trial%d" % i) for i in range(8)]
-        trial_first = keep.tile([P, PACK * NARROW], F32, name="trial_first", align_bytes=64)
+        in_turn = keep.tile([P, 6 * NARROW], F32, name="in_turn", align_bytes=64)
+        trial_first = in_turn[:, 2 * NARROW:]
+        second_flat = trial_first.bitcast(BF16)
+        second_woven = second_flat.rearrange("p (b c t) -> p b c t", b=HP, t=PACK)
+        planes1_back = in_turn[:, :PACK * NARROW].bitcast(BF16).rearrange("p (t c) -> p t c", t=PACK)
+        planes1_second = keep.tile([P, PACK, NARROW], BF16, name="planes1_second")
 
         def load_table(a):
             nc.sync.dma_start(table[a][:], tab_words[a].rearrange("p t i -> p (t i)").bitcast(I32))
@@ -164,8 +168,8 @@ def tile_list_yield_clipped_forces_kernel(tc, tab_words, tab_scales, w1, w2_word
             for t0 in (0, 2):
                 quantize_w1(b, a, t0, t0 + 2)
 
-        def first_product(first_bank, b, a, j0, j1, start, stop):
-            for t in range(PACK):
+        def first_product(first_bank, b, a, j0, j1, start, stop, ts=range(PACK)):
+            for t in ts:
                 nc.tensor.matmul_mx(
                     out=bank[first_bank + t][:, :j1 - j0],
                     lhsT=w1_codes[b, a][:, t * P:(t + 1) * P].bitcast(FP8X4),
@@ -181,8 +185,8 @@ def tile_list_yield_clipped_forces_kernel(tc, tab_words, tab_scales, w1, w2_word
         def drain(first_bank, b, t, dst):
             nc.scalar.activation(dst, bank[first_bank + t][:, :dst.shape[1]], IDENT, bias=row_consts[:, t, b, 0:1])
 
-        def clip(planes, b, t, src):
-            nc.vector.tensor_scalar(planes[:, t, :], src, row_consts[:, t, b, 1:2], row_consts[:, t, b, 2:3], ALU.max, ALU.min)
+        def clip(planes, b, t, src, engine=nc.vector):
+            engine.tensor_scalar(planes[:, t, :], src, row_consts[:, t, b, 2:3], row_consts[:, t, b, 1:2], ALU.min, ALU.max)
 
         def drain_clip(planes, first_bank, b, ts, trials):
             for t in ts:
@@ -197,28 +201,40 @@ def tile_list_yield_clipped_forces_kernel(tc, tab_words, tab_scales, w1, w2_word
             nc.vector.quantize_mx(out=h_codes[b][:, j0:j1].bitcast(FP8X4), scales=h_sc[b][:, j0:j1],
                                   in_=src[:, :PACK * (j1 - j0)])
 
-        def forces(nt, j0, j1, y):
+        def force_bank(nt, j0):
+            return bank[nt if j0 == 0 else (0, 6, 7, 3)[nt]]
+
+        def second_product(nt, j0, j1):
             width = PASS if j1 - j0 == PASS else FP4_N
             for b in range(HP):
-                codes, scales, shift = (second_codes, second_sc, NARROW * (b - 1)) if j0 == NARROW else (h_codes[b], h_sc[b], 0)
+                codes, scales, shift = (second_codes, second_sc, -NARROW * b) if j0 == NARROW else (h_codes[b], h_sc[b], 0)
                 for g in range(j0, j1, width):
                     nc.tensor.matmul_mx(
-                        out=bank[nt][:, g - j0:g - j0 + width],
+                        out=force_bank(nt, j0)[:, g - j0:g - j0 + width],
                         lhsT=w2_codes[:, b, :].bitcast(U8)[:, 2 * nt * P:2 * (nt + 1) * P].bitcast(FP4X4),
                         lhsT_scale=w2_sc[:, b, :].bitcast(U8)[:, nt * P:(nt + 1) * P],
                         rhs=codes[:, g + shift:g + shift + width].bitcast(FP8X4),
                         rhs_scale=scales[:, g + shift:g + shift + width],
                         start=(b == 0 and g == j0), stop=(b == HP - 1 and g == j1 - width))
-            nc.scalar.activation(y, bank[nt][:, :j1 - j0], IDENT, bias=f0_sb[:, nt:nt + 1])
-            nc.vector.tensor_tensor(window[nt][:].indirect(scatter_list[:, j0 // LIST_ROWS:j1 // LIST_ROWS]),
-                                    y, wgo_sb[:, j0:j1], ALU.mult)
+
+        def places(nt, j0, j1):
+            return window[nt][:].indirect(scatter_list[:, j0 // LIST_ROWS:j1 // LIST_ROWS])
+
+        def forces(nt, j0, j1, y, product=None):
+            second_product(nt, j0, j1)
+            nc.scalar.activation(y, force_bank(nt, j0)[:, :j1 - j0], IDENT, bias=f0_sb[:, nt:nt + 1])
+            if product is None:
+                nc.vector.tensor_tensor(places(nt, j0, j1), y, wgo_sb[:, j0:j1], ALU.mult)
+            else:
+                nc.gpsimd.tensor_tensor(product, y, wgo_sb[:, j0:j1], ALU.mult)
+                nc.vector.tensor_copy(places(nt, j0, j1), product)
 
         def y_on_stage(a, word0):
             return stage_flat[a].bitcast(F32)[:, word0:word0 + NARROW]
 
         front = [trial[t][:] for t in range(PACK)]
         back = [trial[PACK + t][:] for t in range(PACK)]
-        back_narrow = [trial[PACK + t][:, :NARROW] for t in range(PACK)]
+        front_narrow = [trial[t][:, :NARROW] for t in range(PACK)]
         first = [trial_first[:, NARROW * t:NARROW * (t + 1)] for t in range(PACK)]
         lower = [woven[a][:, :NARROW, :] for a in range(KP)]
         upper = [woven[a][:, NARROW:, :] for a in range(KP)]
@@ -276,30 +292,42 @@ def tile_list_yield_clipped_forces_kernel(tc, tab_words, tab_scales, w1, w2_word
         quantize_h(woven0_first, 0, r0, r1)
         for t in range(PACK):
             clip(planes0_back, 0, t, back[t])
-        all_passes(4, 1, r1, r3)
-        drain_clip(planes1_mid, 4, 1, range(PACK), front)
-        forces(0, r0, r1, y_sb[0][:, r0:r1])
-        forces(1, r0, r1, y_sb[1][:, r0:r1])
+        all_passes(4, 1, r1, r2)
+        drain_clip(planes1_second, 4, 1, range(PACK), front_narrow)
+        second_product(0, r0, r1)
+        nc.vector.scalar_tensor_tensor(first_weighted[:], bank[0][:, :NARROW], f0_sb[:, 0:1], wgo_sb[:, r0:r1], ALU.add, ALU.mult)
+        nc.vector.tensor_copy(places(0, r0, r1), first_weighted[:])
+        forces(1, r0, r1, in_turn[:, 3 * NARROW // 2:5 * NARROW // 2], y_on_stage(0, 0))
+        forces(2, r0, r1, y_sb[2][:, r0:r1], y_on_stage(0, 2 * NARROW))
 
-        all_passes(4, 1, r3, S)
-        drain_clip(planes1_last, 4, 1, range(2), back_narrow)
-        weave(on_scalar, upper[1], planes1_mid, 0)
-        weave(on_scalar, lower[1], planes0_front, NARROW)
-        nc.vector.quantize_mx(out=second_codes[:].bitcast(FP8X4), scales=second_sc[:], in_=stage_flat[1])
-        forces(2, r0, r1, y_on_stage(0, 3 * NARROW // 2))
-        drain_clip(planes1_last, 4, 1, range(2, PACK), back_narrow)
-        forces(3, r0, r1, y_on_stage(1, 3 * NARROW // 2))
+        def drain_clip_back(t, bank_number):
+            for a in range(KP):
+                first_product(bank_number - t, 1, a, r2, S, a == 0, a == KP - 1, [t])
+            drain(bank_number - t, 1, t, back[t])
+            clip(planes1_back, 1, t, back[t], nc.gpsimd)
+
+        def y_on_planes(planes):
+            return planes.rearrange("p t c -> p (t c)").bitcast(F32)[:, :NARROW]
+
+        weave(on_scalar, second_woven[:, 1, :, :], planes0_front, NARROW)
+        weave(on_scalar, second_woven[:, 0, :, :], planes1_second, 0)
+        nc.vector.quantize_mx(out=second_codes[:].bitcast(FP8X4), scales=second_sc[:], in_=second_flat)
+        drain_clip_back(1, 4)
+        forces(3, r0, r1, y_sb[3][:, r0:r1], y_on_planes(planes1_second[:]))
+        drain_clip_back(0, 5)
+        drain_clip_back(2, 1)
+        drain_clip_back(3, 2)
 
         forces(0, r1, r2, y_sb[0][:, r1:r2])
-        weave(on_scalar, lower[2], planes1_mid, NARROW)
-        weave(on_scalar, upper[2], planes1_last, 0)
-        quantize_h(stage_flat[2], 1, r2, S)
-        forces(1, r1, r2, y_sb[1][:, r1:r2])
         weave(on_scalar, lower[0], planes0_back, 0)
         weave(on_scalar, upper[0], planes0_back, NARROW)
         quantize_h(stage_flat[0], 0, r2, S)
-        forces(2, r1, r2, y_on_stage(2, 0))
-        forces(3, r1, r2, y_on_stage(0, 0))
+        forces(1, r1, r2, y_sb[1][:, r1:r2])
+        weave(on_scalar, lower[2], planes1_back, 0)
+        forces(2, r1, r2, y_sb[2][:, r1:r2])
+        weave(on_scalar, upper[2], planes1_back, NARROW)
+        quantize_h(stage_flat[2], 1, r2, S)
+        forces(3, r1, r2, y_on_planes(planes1_back))
 
         for nt in range(NT):
             forces(nt, r2, S, y_sb[nt][:, r2:])

@@ -91,8 +91,8 @@ def tile_list_yield_clipped_forces_kernel(tc, tab_words, tab_scales, w1, w2_word
         planes1_first = keep.tile([P, PACK, NARROW], BF16, name="planes1_first")
         first_weighted = keep.tile([P, NARROW], F32, name="first_weighted")
         trial = [keep.tile([P, PASS], F32, name="trial%d" % i) for i in range(8)]
-        in_turn = keep.tile([P, 6 * NARROW], F32, name="in_turn", align_bytes=64)
-        trial_first = in_turn[:, 2 * NARROW:]
+        in_turn = keep.tile([P, 8 * NARROW], F32, name="in_turn", align_bytes=64)
+        trial_first = in_turn[:, 4 * NARROW:]
         second_flat = trial_first.bitcast(BF16)
         second_woven = second_flat.rearrange("p (b c t) -> p b c t", b=HP, t=PACK)
         planes1_back = in_turn[:, :PACK * NARROW].bitcast(BF16).rearrange("p (t c) -> p t c", t=PACK)
@@ -202,7 +202,7 @@ def tile_list_yield_clipped_forces_kernel(tc, tab_words, tab_scales, w1, w2_word
                                   in_=src[:, :PACK * (j1 - j0)])
 
         def force_bank(nt, j0):
-            return bank[nt if j0 == 0 else (0, 6, 7, 3)[nt]]
+            return bank[nt if j0 == 0 else (1, 6, 7, 3)[nt]]
 
         def second_product(nt, j0, j1):
             width = PASS if j1 - j0 == PASS else FP4_N
@@ -294,17 +294,20 @@ def tile_list_yield_clipped_forces_kernel(tc, tab_words, tab_scales, w1, w2_word
             clip(planes0_back, 0, t, back[t])
         all_passes(4, 1, r1, r2)
         drain_clip(planes1_second, 4, 1, range(PACK), front_narrow)
-        second_product(0, r0, r1)
-        nc.vector.scalar_tensor_tensor(first_weighted[:], bank[0][:, :NARROW], f0_sb[:, 0:1], wgo_sb[:, r0:r1], ALU.add, ALU.mult)
-        nc.vector.tensor_copy(places(0, r0, r1), first_weighted[:])
-        forces(1, r0, r1, in_turn[:, 3 * NARROW // 2:5 * NARROW // 2], y_on_stage(0, 0))
-        forces(2, r0, r1, y_sb[2][:, r0:r1], y_on_stage(0, 2 * NARROW))
+        first_products = (first_weighted[:], y_sb[1][:, r0:r1])
+        for nt, product in enumerate(first_products):
+            second_product(nt, r0, r1)
+            nc.vector.scalar_tensor_tensor(product, bank[nt][:, :NARROW], f0_sb[:, nt:nt + 1], wgo_sb[:, r0:r1],
+                                           ALU.add, ALU.mult)
+        for nt, product in enumerate(first_products):
+            nc.vector.tensor_copy(places(nt, r0, r1), product)
+        forces(2, r0, r1, in_turn[:, 7 * NARROW // 2:9 * NARROW // 2], y_on_stage(0, 3 * NARROW // 2))
 
-        def drain_clip_back(t, bank_number):
+        def drain_clip_back(t, bank_number, engine):
             for a in range(KP):
                 first_product(bank_number - t, 1, a, r2, S, a == 0, a == KP - 1, [t])
             drain(bank_number - t, 1, t, back[t])
-            clip(planes1_back, 1, t, back[t], nc.gpsimd)
+            clip(planes1_back, 1, t, back[t], engine)
 
         def y_on_planes(planes):
             return planes.rearrange("p t c -> p (t c)").bitcast(F32)[:, :NARROW]
@@ -312,11 +315,11 @@ def tile_list_yield_clipped_forces_kernel(tc, tab_words, tab_scales, w1, w2_word
         weave(on_scalar, second_woven[:, 1, :, :], planes0_front, NARROW)
         weave(on_scalar, second_woven[:, 0, :, :], planes1_second, 0)
         nc.vector.quantize_mx(out=second_codes[:].bitcast(FP8X4), scales=second_sc[:], in_=second_flat)
-        drain_clip_back(1, 4)
-        forces(3, r0, r1, y_sb[3][:, r0:r1], y_on_planes(planes1_second[:]))
-        drain_clip_back(0, 5)
-        drain_clip_back(2, 1)
-        drain_clip_back(3, 2)
+        drain_clip_back(0, 4, nc.gpsimd)
+        drain_clip_back(3, 5, nc.gpsimd)
+        drain_clip_back(1, 0, nc.gpsimd)
+        forces(3, r0, r1, y_on_planes(planes1_second[:]))
+        drain_clip_back(2, 2, nc.vector)
 
         forces(0, r1, r2, y_sb[0][:, r1:r2])
         weave(on_scalar, lower[0], planes0_back, 0)

@@ -28,9 +28,9 @@ QUADRANTS = 4
 NARROW = 256
 FP4_N = 128
 HALVED = ((1, 0), (1, 2))
-SCALAR_SHARE_01 = 72
-SCALAR_SHARE_02 = 36
-SCALAR_SHARE_10 = 44
+SCALAR_SHARE_01 = 80
+SCALAR_SHARE_02 = 44
+SCALAR_SHARE_10 = 36
 
 
 def tile_list_yield_clipped_forces_kernel(tc, tab_words, tab_scales, w1, w2_words, w2_scales,
@@ -116,8 +116,8 @@ def tile_list_yield_clipped_forces_kernel(tc, tab_words, tab_scales, w1, w2_word
         nc.vector.memset(vec_rows[:], 0.0)
         nc.vector.memset(w2_sc[:], 0)
         make_identity(nc, identity[:])
-        nc.sync.dma_start(gather_list[:], offs)
         load_table(0)
+        nc.sync.dma_start(gather_list[:], offs)
         load_table(1)
         for q in (0, 2, 1, 3):
             nc.gpsimd.dma_start(table_sc[32 * q:32 * q + 4 * KP, :], tab_scales[:, 4 * q:4 * q + 4, :].bitcast(I32))
@@ -125,8 +125,8 @@ def tile_list_yield_clipped_forces_kernel(tc, tab_words, tab_scales, w1, w2_word
             nc.sync.dma_start(vec_rows[4 * i:P:64, :], vec.rearrange("(b c) -> b c", b=HP))
         nc.sync.dma_start(vec_rows[f0_rows, :P], f0.rearrange("(n p) -> n p", p=P))
         load_w2_scales(0)
-        load_w2_scales(1)
         load_w1(0, 0)
+        load_w2_scales(1)
         load_table(2)
         load_w1(0, 1)
         load_w1(0, 2)

@@ -160,7 +160,8 @@ def tile_list_yield_clipped_forces_kernel(tc, tab_words, tab_scales, w1, w2_word
 
         def quantize_w1(b, a, t0, t1):
             nc.vector.quantize_mx(out=w1_codes[b, a][:, t0 * P:t1 * P].bitcast(FP8X4),
-                                  scales=w1_sc[b, a][:, t0 * P:t1 * P], in_=rounded(b, a).rearrange("p t m j -> p (t m j)")[:, PASS * t0:PASS * t1])
+                                  scales=w1_sc[b, a][:, t0 * P:t1 * P],
+                                  in_=rounded(b, a).rearrange("p t m j -> p (t m j)")[:, PASS * t0:PASS * t1])
 
         def round_in_pairs(b, a, m0):
             for t0 in (0, 2):
@@ -186,7 +187,8 @@ def tile_list_yield_clipped_forces_kernel(tc, tab_words, tab_scales, w1, w2_word
             nc.scalar.activation(dst, bank[first_bank + t][:, :dst.shape[1]], IDENT, bias=row_consts[:, t, b, 0:1])
 
         def clip(planes, b, t, src, engine=nc.vector):
-            engine.tensor_scalar(planes[:, t, :], src, row_consts[:, t, b, 2:3], row_consts[:, t, b, 1:2], ALU.min, ALU.max)
+            engine.tensor_scalar(planes[:, t, :], src, row_consts[:, t, b, 2:3], row_consts[:, t, b, 1:2],
+                                 ALU.min, ALU.max)
 
         def drain_clip(planes, first_bank, b, ts, trials):
             for t in ts:
@@ -202,12 +204,13 @@ def tile_list_yield_clipped_forces_kernel(tc, tab_words, tab_scales, w1, w2_word
                                   in_=src[:, :PACK * (j1 - j0)])
 
         def force_bank(nt, j0):
-            return bank[nt if j0 == 0 else (1, 6, 7, 3)[nt]]
+            return bank[nt if j0 in (0, 3 * NARROW) else (1, 6, 7, 3)[nt]]
 
         def second_product(nt, j0, j1):
             width = PASS if j1 - j0 == PASS else FP4_N
             for b in range(HP):
-                codes, scales, shift = (second_codes, second_sc, -NARROW * b) if j0 == NARROW else (h_codes[b], h_sc[b], 0)
+                codes, scales, shift = ((second_codes, second_sc, -NARROW * b) if j0 == NARROW
+                                        else (h_codes[b], h_sc[b], 0))
                 for g in range(j0, j1, width):
                     nc.tensor.matmul_mx(
                         out=force_bank(nt, j0)[:, g - j0:g - j0 + width],
@@ -229,8 +232,8 @@ def tile_list_yield_clipped_forces_kernel(tc, tab_words, tab_scales, w1, w2_word
                 nc.gpsimd.tensor_tensor(product, y, wgo_sb[:, j0:j1], ALU.mult)
                 nc.vector.tensor_copy(places(nt, j0, j1), product)
 
-        def y_on_stage(a, word0):
-            return stage_flat[a].bitcast(F32)[:, word0:word0 + NARROW]
+        def y_on_planes(planes):
+            return planes.rearrange("p t c -> p (t c)").bitcast(F32)[:, :NARROW]
 
         front = [trial[t][:] for t in range(PACK)]
         back = [trial[PACK + t][:] for t in range(PACK)]
@@ -301,16 +304,15 @@ def tile_list_yield_clipped_forces_kernel(tc, tab_words, tab_scales, w1, w2_word
                                            ALU.add, ALU.mult)
         for nt, product in enumerate(first_products):
             nc.vector.tensor_copy(places(nt, r0, r1), product)
-        forces(2, r0, r1, in_turn[:, 7 * NARROW // 2:9 * NARROW // 2], y_on_stage(0, 3 * NARROW // 2))
+        across_units = in_turn[:, 7 * NARROW // 2:9 * NARROW // 2]
+        across_ranges = stage_flat[0].bitcast(F32)[:, 3 * NARROW // 2:5 * NARROW // 2]
+        forces(2, r0, r1, across_units, across_ranges)
 
         def drain_clip_back(t, bank_number, engine):
             for a in range(KP):
                 first_product(bank_number - t, 1, a, r2, S, a == 0, a == KP - 1, [t])
             drain(bank_number - t, 1, t, back[t])
             clip(planes1_back, 1, t, back[t], engine)
-
-        def y_on_planes(planes):
-            return planes.rearrange("p t c -> p (t c)").bitcast(F32)[:, :NARROW]
 
         weave(on_scalar, second_woven[:, 1, :, :], planes0_front, NARROW)
         weave(on_scalar, second_woven[:, 0, :, :], planes1_second, 0)
@@ -332,6 +334,7 @@ def tile_list_yield_clipped_forces_kernel(tc, tab_words, tab_scales, w1, w2_word
         quantize_h(stage_flat[2], 1, r2, S)
         forces(3, r1, r2, y_on_planes(planes1_back))
 
-        for nt in range(NT):
-            forces(nt, r2, S, y_sb[nt][:, r2:])
+        forces(0, r2, r3, y_sb[0][:, r2:r3])
+        for nt, j0 in ((1, r2), (0, r3), (2, r2), (3, r2)):
+            forces(nt, j0, S, y_sb[nt][:, j0:])
             nc.sync.dma_start(out[nt * P:(nt + 1) * P, :], window[nt][:])

@@ -71,7 +71,7 @@ def tile_list_yield_clipped_forces_kernel(tc, tab_words, tab_scales, w1, w2_word
                 w1_sc[b, a] = keep.tile([P, PASS], U8, name="w1_sc%d%d" % (b, a), align_bytes=64)
         w2_codes = keep.tile([P, HP, N // 2], I32, name="w2_codes", align_bytes=64)
         w2_sc = keep.tile([P, HP, N // 4], I32, name="w2_sc", align_bytes=64)
-        f0_rows = slice(12, P, 32)
+        f0_rows = slice(28, P, 32)
         vec_rows = keep.tile([P, PASS], F32, name="vec_rows", tag="vec_rows", align_bytes=64)
         identity = keep.tile([P, P], F32, name="identity")
         row_consts = keep.tile([P, PACK, HP, 3], F32, name="row_consts")
@@ -88,7 +88,9 @@ def tile_list_yield_clipped_forces_kernel(tc, tab_words, tab_scales, w1, w2_word
         first_stage = keep.tile([P, PACK, P, PACK], BF16, name="first_stage", tag="first_stage", align_bytes=64)
         woven = [stage[a][:].rearrange("p t m j -> p (t m) j") for a in range(KP)]
         stage_flat = [stage[a][:].rearrange("p t m j -> p (t m j)") for a in range(KP)]
-        planes1_first = keep.tile([P, PACK, NARROW], BF16, name="planes1_first")
+        planes1_front = keep.tile([P, (PACK + 1) * NARROW], BF16, name="planes1_front")
+        planes1_first = planes1_front[:, NARROW:].rearrange("p (t c) -> p t c", t=PACK)
+        planes1_second = planes1_front[:, :PACK * NARROW].rearrange("p (t c) -> p t c", t=PACK)
         first_weighted = keep.tile([P, NARROW], F32, name="first_weighted")
         trial = [keep.tile([P, PASS], F32, name="trial%d" % i) for i in range(8)]
         in_turn = keep.tile([P, 8 * NARROW], F32, name="in_turn", align_bytes=64)
@@ -96,7 +98,6 @@ def tile_list_yield_clipped_forces_kernel(tc, tab_words, tab_scales, w1, w2_word
         second_flat = trial_first.bitcast(BF16)
         second_woven = second_flat.rearrange("p (b c t) -> p b c t", b=HP, t=PACK)
         planes1_back = in_turn[:, :PACK * NARROW].bitcast(BF16).rearrange("p (t c) -> p t c", t=PACK)
-        planes1_second = keep.tile([P, PACK, NARROW], BF16, name="planes1_second")
 
         def load_table(a):
             nc.sync.dma_start(table[a][:], tab_words[a].rearrange("p t i -> p (t i)").bitcast(I32))
@@ -120,20 +121,20 @@ def tile_list_yield_clipped_forces_kernel(tc, tab_words, tab_scales, w1, w2_word
         nc.sync.dma_start(gather_list[:], offs)
         load_table(1)
         for q in (0, 2, 1, 3):
-            nc.gpsimd.dma_start(table_sc[32 * q:32 * q + 4 * KP, :], tab_scales[:, 4 * q:4 * q + 4, :].bitcast(I32))
+            nc.gpsimd.dma_start(table_sc[32 * q + 4:32 * q + 4 + 4 * KP, :], tab_scales[:, 4 * q:4 * q + 4, :].bitcast(I32))
         for i, vec in enumerate((s0, lo, hi)):
-            nc.sync.dma_start(vec_rows[4 * i:P:64, :], vec.rearrange("(b c) -> b c", b=HP))
+            nc.sync.dma_start(vec_rows[16 + 4 * i:P:64, :], vec.rearrange("(b c) -> b c", b=HP))
         nc.sync.dma_start(vec_rows[f0_rows, :P], f0.rearrange("(n p) -> n p", p=P))
         load_w2_scales(0)
         load_w1(0, 0)
-        load_w2_scales(1)
+        load_w2_scales(2)
         load_table(2)
         load_w1(0, 1)
         load_w1(0, 2)
         for a in range(KP):
             load_w1(1, a)
         nc.sync.dma_start(w2_codes[:], w2_words.rearrange("a p c -> p a c").bitcast(I32))
-        for q in range(2, QUADRANTS):
+        for q in (1, 3):
             load_w2_scales(q)
         nc.sync.dma_start(scatter_list[:], offs2)
         nc.sync.dma_start(wgo_sb[:], wgo)
@@ -176,7 +177,7 @@ def tile_list_yield_clipped_forces_kernel(tc, tab_words, tab_scales, w1, w2_word
                     lhsT=w1_codes[b, a][:, t * P:(t + 1) * P].bitcast(FP8X4),
                     lhsT_scale=w1_sc[b, a][:, t * P:(t + 1) * P],
                     rhs=v_codes[a][:, j0:j1].bitcast(FP8X4),
-                    rhs_scale=v_sc[4 * a:, j0:j1],
+                    rhs_scale=v_sc[4 * a + 4:, j0:j1],
                     start=start, stop=stop)
 
         def all_passes(first_bank, b, j0, j1):
@@ -246,7 +247,7 @@ def tile_list_yield_clipped_forces_kernel(tc, tab_words, tab_scales, w1, w2_word
         for t in range(PACK):
             nc.tensor.transpose(bank[0][:, t * P:(t + 1) * P], vec_rows[:, t:PASS:PACK], identity[:])
         nc.tensor.transpose(bank[1][:, :P], vec_rows[:, :P], identity[:])
-        nc.scalar.copy(row_consts[:], bank[0][:].rearrange("p (t b r) -> p t b r", t=PACK, b=HP)[:, :, :, 0:12:4])
+        nc.scalar.copy(row_consts[:], bank[0][:].rearrange("p (t b r) -> p t b r", t=PACK, b=HP)[:, :, :, 16:28:4])
         nc.scalar.copy(f0_sb[:], bank[1][:, f0_rows])
 
         gather_words(0)
@@ -319,8 +320,8 @@ def tile_list_yield_clipped_forces_kernel(tc, tab_words, tab_scales, w1, w2_word
         nc.vector.quantize_mx(out=second_codes[:].bitcast(FP8X4), scales=second_sc[:], in_=second_flat)
         drain_clip_back(0, 4, nc.gpsimd)
         drain_clip_back(3, 5, nc.gpsimd)
-        drain_clip_back(1, 0, nc.gpsimd)
-        forces(3, r0, r1, y_on_planes(planes1_second[:]))
+        drain_clip_back(1, 6, nc.gpsimd)
+        forces(3, r0, r1, y_on_planes(planes1_second))
         drain_clip_back(2, 2, nc.vector)
 
         forces(0, r1, r2, y_sb[0][:, r1:r2])

from contextlib import ExitStack

import concourse.mybir as mybir
from concourse.masks import make_identity

K, H, N, T, S, T2 = 1536, 1024, 512, 2048, 1024, 2048
FLOPS = 2 * K * H * S + 2 * H * N * S

F32 = mybir.dt.float32
BF16 = mybir.dt.bfloat16
I32 = mybir.dt.int32
U32 = mybir.dt.uint32
U16 = mybir.dt.uint16
U8 = mybir.dt.uint8
FP8X4 = mybir.dt.float8_e4m3fn_x4
FP4X4 = mybir.dt.float4_e2m1fn_x4
ALU = mybir.AluOpType
IDENT = mybir.ActivationFunctionType.Identity

P = 128
PACK = 4
PASS = P * PACK
KP = K // PASS
HP = H // PASS
NT = N // P
LIST_ROWS = 16
QUADRANTS = 4
NARROW = 256
FP4_N = 128
HALVED = ((1, 0), (1, 2))
SCALAR_SHARE_01 = 80
SCALAR_SHARE_02 = 44
SCALAR_SHARE_10 = 36


def tile_list_yield_clipped_forces_kernel(tc, tab_words, tab_scales, w1, w2_words, w2_scales,
                                                      s0, lo, hi, f0, wgo, offs, offs2, out):
    nc = tc.nc
    with ExitStack() as ctx:
        keep = ctx.enter_context(tc.tile_pool(name="keep", bufs=1))
        psum = ctx.enter_context(tc.psum_pool(name="psum", bufs=1))

        gather_list = keep.tile([P, S // LIST_ROWS], U16, name="gather_list")
        scatter_list = keep.tile([P, S // LIST_ROWS], U16, name="scatter_list")
        table = [keep.tile([P, T], I32, name="table%d" % a, tag="table%d" % a, align_bytes=64) for a in range(KP)]
        table_sc = keep.tile([P, T // 4], I32, name="table_sc")
        v_codes = [keep.tile([P, S], U32, name="v_codes%d" % a, align_bytes=64) for a in range(KP)]

        plane_words = PASS // 2
        piece_words = PACK * PASS
        planes0_front = keep.tile([P, PACK, PASS], BF16, name="planes0_front")
        under_back = keep.tile([P, piece_words + piece_words // 2], F32, name="under_back", align_bytes=64)
        under_first = keep.tile([P, piece_words // 2], F32, name="under_first", align_bytes=64)
        planes0_back = under_back[:, piece_words - 2 * plane_words:piece_words + 2 * plane_words].bitcast(BF16).rearrange(
            "p (t c) -> p t c", t=PACK)
        woven0_first = under_first[:, :PACK * NARROW // 2].bitcast(BF16)

        w1_raw = {(1, 1): [under_back[:, :piece_words].rearrange("p (j c) -> p j c", j=PACK)],
                  (1, 2): [under_first[:].rearrange("p (j c) -> p j c", j=PACK),
                           under_back[:, piece_words:].rearrange("p (j c) -> p j c", j=PACK)]}
        w1_codes = {}
        w1_sc = {}
        for b in range(HP):
            for a in range(KP):
                parts = 2 if (b, a) in HALVED else 1
                loaded = w1_raw.setdefault((b, a), [])
                for part in range(len(loaded), parts):
                    loaded.append(keep.tile([P, PACK, PASS // parts], F32, name="w1_raw%d%d_%d" % (b, a, part),
                                            align_bytes=64)[:])
                w1_codes[b, a] = keep.tile([P, PASS], U32, name="w1_codes%d%d" % (b, a), align_bytes=64)
                w1_sc[b, a] = keep.tile([P, PASS], U8, name="w1_sc%d%d" % (b, a), align_bytes=64)
        w2_codes = keep.tile([P, HP, N // 2], I32, name="w2_codes", align_bytes=64)
        w2_sc = keep.tile([P, HP, N // 4], I32, name="w2_sc", align_bytes=64)
        f0_rows = slice(28, P, 32)
        vec_rows = keep.tile([P, PASS], F32, name="vec_rows", tag="vec_rows", align_bytes=64)
        identity = keep.tile([P, P], F32, name="identity")
        row_consts = keep.tile([P, PACK, HP, 3], F32, name="row_consts")
        f0_sb = keep.tile([P, NT], F32, name="f0_sb")
        wgo_sb = keep.tile([P, S], F32, name="wgo_sb")
        h_codes = [keep.tile([P, S], U32, name="h_codes%d" % b, align_bytes=64) for b in range(HP)]
        h_sc = [keep.tile([P, S], U8, name="h_sc%d" % b, align_bytes=64) for b in range(HP)]
        second_codes = keep.tile([P, HP * NARROW], U32, name="second_codes", align_bytes=64)
        second_sc = keep.tile([P, HP * NARROW], U8, name="second_sc", align_bytes=64)
        y_sb = [keep.tile([P, S], F32, name="y_sb%d" % nt) for nt in range(NT)]
        window = [keep.tile([P, T2], F32, name="window0")]
        bank = [psum.tile([P, PASS], F32, name="bank%d" % i) for i in range(8)]
        stage = [keep.tile([P, PACK, P, PACK], BF16, name="w1_stage%d" % a, align_bytes=64) for a in range(KP)]
        first_stage = keep.tile([P, PACK, P, PACK], BF16, name="first_stage", tag="first_stage", align_bytes=64)
        woven = [stage[a][:].rearrange("p t m j -> p (t m) j") for a in range(KP)]
        stage_flat = [stage[a][:].rearrange("p t m j -> p (t m j)") for a in range(KP)]
        planes1_front = keep.tile([P, (PACK + 1) * NARROW], BF16, name="planes1_front")
        planes1_first = planes1_front[:, NARROW:].rearrange("p (t c) -> p t c", t=PACK)
        planes1_second = planes1_front[:, :PACK * NARROW].rearrange("p (t c) -> p t c", t=PACK)
        first_weighted = keep.tile([P, NARROW], F32, name="first_weighted")
        trial = [keep.tile([P, PASS], F32, name="trial%d" % i) for i in range(8)]
        in_turn = keep.tile([P, 8 * NARROW], F32, name="in_turn", align_bytes=64)
        trial_first = in_turn[:, 4 * NARROW:]
        second_flat = trial_first.bitcast(BF16)
        second_woven = second_flat.rearrange("p (b c t) -> p b c t", b=HP, t=PACK)
        planes1_back = in_turn[:, :PACK * NARROW].bitcast(BF16).rearrange("p (t c) -> p t c", t=PACK)

        def load_table(a):
            nc.sync.dma_start(table[a][:], tab_words[a].rearrange("p t i -> p (t i)").bitcast(I32))

        def load_w1(b, a):
            width = PASS // len(w1_raw[b, a])
            for part, raw in enumerate(w1_raw[b, a]):
                c0 = b * PASS + part * width
                nc.sync.dma_start(
                    raw, w1[a * PASS:(a + 1) * PASS, c0:c0 + width].rearrange("(p j) c -> p j c", j=PACK))

        def load_w2_scales(q):
            nc.sync.dma_start(w2_sc[32 * q:32 * q + 4, :, :],
                              w2_scales[:, 4 * q:4 * q + 4, :].rearrange("a r n -> r a n").bitcast(I32))

        nc.gpsimd.memset(table_sc[:], 0)
        nc.vector.memset(vec_rows[:], 0.0)
        nc.vector.memset(w2_sc[:], 0)
        make_identity(nc, identity[:])
        load_table(0)
        nc.sync.dma_start(gather_list[:], offs)
        load_table(1)
        for q in (0, 2, 1, 3):
            nc.gpsimd.dma_start(table_sc[32 * q + 4:32 * q + 4 + 4 * KP, :], tab_scales[:, 4 * q:4 * q + 4, :].bitcast(I32))
        for i, vec in enumerate((s0, lo, hi)):
            nc.sync.dma_start(vec_rows[16 + 4 * i:P:64, :], vec.rearrange("(b c) -> b c", b=HP))
        nc.sync.dma_start(vec_rows[f0_rows, :P], f0.rearrange("(n p) -> n p", p=P))
        load_w2_scales(0)
        load_w1(0, 0)
        load_w2_scales(2)
        load_table(2)
        load_w1(0, 1)
        load_w1(0, 2)
        for a in range(KP):
            load_w1(1, a)
        nc.sync.dma_start(w2_codes[:], w2_words.rearrange("a p c -> p a c").bitcast(I32))
        for q in (1, 3):
            load_w2_scales(q)
        nc.sync.dma_start(scatter_list[:], offs2)
        nc.sync.dma_start(wgo_sb[:], wgo)
        nc.vector.memset(window[0][:], 0.0)

        def zero_window(under):
            window.append(keep.tile([P, T2], F32, name="window%d" % len(window), tag=under, align_bytes=64))
            nc.gpsimd.memset(window[-1][:], 0.0)

        def gather_words(a):
            nc.vector.tensor_copy(v_codes[a][:], table[a][:].bitcast(U32).indirect(gather_list[:]))

        on_vector, on_scalar = nc.vector.tensor_copy, nc.scalar.copy

        def rounded(b, a):
            return first_stage[:] if (b, a) == (0, 0) else stage[a][:]

        def round_w1(b, a, copier, m0, m1, t0=0, t1=PACK):
            groups = P // len(w1_raw[b, a])
            part = m0 // groups
            src = w1_raw[b, a][part].rearrange("p j (m t) -> p m j t", t=PACK)
            dst = rounded(b, a).rearrange("p t m j -> p m j t")
            copier(dst[:, m0:m1, :, t0:t1], src[:, m0 - part * groups:m1 - part * groups, :, t0:t1])

        def quantize_w1(b, a, t0, t1):
            nc.vector.quantize_mx(out=w1_codes[b, a][:, t0 * P:t1 * P].bitcast(FP8X4),
                                  scales=w1_sc[b, a][:, t0 * P:t1 * P],
                                  in_=rounded(b, a).rearrange("p t m j -> p (t m j)")[:, PASS * t0:PASS * t1])

        def round_in_pairs(b, a, m0):
            for t0 in (0, 2):
                round_w1(b, a, on_vector, m0, P, t0, t0 + 2)
            for t0 in (0, 2):
                quantize_w1(b, a, t0, t0 + 2)

        def first_product(first_bank, b, a, j0, j1, start, stop, ts=range(PACK)):
            for t in ts:
                nc.tensor.matmul_mx(
                    out=bank[first_bank + t][:, :j1 - j0],
                    lhsT=w1_codes[b, a][:, t * P:(t + 1) * P].bitcast(FP8X4),
                    lhsT_scale=w1_sc[b, a][:, t * P:(t + 1) * P],
                    rhs=v_codes[a][:, j0:j1].bitcast(FP8X4),
                    rhs_scale=v_sc[4 * a + 4:, j0:j1],
                    start=start, stop=stop)

        def all_passes(first_bank, b, j0, j1):
            for a in range(KP):
                first_product(first_bank, b, a, j0, j1, a == 0, a == KP - 1)

        def drain(first_bank, b, t, dst):
            nc.scalar.activation(dst, bank[first_bank + t][:, :dst.shape[1]], IDENT, bias=row_consts[:, t, b, 0:1])

        def clip(planes, b, t, src, engine=nc.vector):
            engine.tensor_scalar(planes[:, t, :], src, row_consts[:, t, b, 2:3], row_consts[:, t, b, 1:2],
                                 ALU.min, ALU.max)

        def drain_clip(planes, first_bank, b, ts, trials):
            for t in ts:
                drain(first_bank, b, t, trials[t])
                clip(planes, b, t, trials[t])

        def weave(copier, dst, planes, c0):
            copier(dst.rearrange("p (c i) t -> p c t i", i=4),
                   planes[:, :, c0:c0 + NARROW].rearrange("p t (c i) -> p c t i", i=4))

        def quantize_h(src, b, j0, j1):
            nc.vector.quantize_mx(out=h_codes[b][:, j0:j1].bitcast(FP8X4), scales=h_sc[b][:, j0:j1],
                                  in_=src[:, :PACK * (j1 - j0)])

        def force_bank(nt, j0):
            return bank[nt if j0 in (0, 3 * NARROW) else (1, 6, 7, 3)[nt]]

        def second_product(nt, j0, j1):
            width = PASS if j1 - j0 == PASS else FP4_N
            for b in range(HP):
                codes, scales, shift = ((second_codes, second_sc, -NARROW * b) if j0 == NARROW
                                        else (h_codes[b], h_sc[b], 0))
                for g in range(j0, j1, width):
                    nc.tensor.matmul_mx(
                        out=force_bank(nt, j0)[:, g - j0:g - j0 + width],
                        lhsT=w2_codes[:, b, :].bitcast(U8)[:, 2 * nt * P:2 * (nt + 1) * P].bitcast(FP4X4),
                        lhsT_scale=w2_sc[:, b, :].bitcast(U8)[:, nt * P:(nt + 1) * P],
                        rhs=codes[:, g + shift:g + shift + width].bitcast(FP8X4),
                        rhs_scale=scales[:, g + shift:g + shift + width],
                        start=(b == 0 and g == j0), stop=(b == HP - 1 and g == j1 - width))

        def places(nt, j0, j1):
            return window[nt][:].indirect(scatter_list[:, j0 // LIST_ROWS:j1 // LIST_ROWS])

        def forces(nt, j0, j1, y, product=None):
            second_product(nt, j0, j1)
            nc.scalar.activation(y, force_bank(nt, j0)[:, :j1 - j0], IDENT, bias=f0_sb[:, nt:nt + 1])
            if product is None:
                nc.vector.tensor_tensor(places(nt, j0, j1), y, wgo_sb[:, j0:j1], ALU.mult)
            else:
                nc.gpsimd.tensor_tensor(product, y, wgo_sb[:, j0:j1], ALU.mult)
                nc.vector.tensor_copy(places(nt, j0, j1), product)

        def y_on_planes(planes):
            return planes.rearrange("p t c -> p (t c)").bitcast(F32)[:, :NARROW]

        front = [trial[t][:] for t in range(PACK)]
        back = [trial[PACK + t][:] for t in range(PACK)]
        front_narrow = [trial[t][:, :NARROW] for t in range(PACK)]
        first = [trial_first[:, NARROW * t:NARROW * (t + 1)] for t in range(PACK)]
        lower = [woven[a][:, :NARROW, :] for a in range(KP)]
        upper = [woven[a][:, NARROW:, :] for a in range(KP)]
        r0, r1, r2, r3 = 0, NARROW, 2 * NARROW, 3 * NARROW

        for t in range(PACK):
            nc.tensor.transpose(bank[0][:, t * P:(t + 1) * P], vec_rows[:, t:PASS:PACK], identity[:])
        nc.tensor.transpose(bank[1][:, :P], vec_rows[:, :P], identity[:])
        nc.scalar.copy(row_consts[:], bank[0][:].rearrange("p (t b r) -> p t b r", t=PACK, b=HP)[:, :, :, 16:28:4])
        nc.scalar.copy(f0_sb[:], bank[1][:, f0_rows])

        gather_words(0)
        zero_window("table0")
        zero_window("vec_rows")
        gather_words(1)
        v_sc = keep.tile([P, S], U8, name="v_sc", tag="table1", align_bytes=64)
        nc.vector.tensor_copy(v_sc[:], table_sc[:].bitcast(U8).indirect(gather_list[:]))
        round_w1(0, 0, on_scalar, 0, P)
        quantize_w1(0, 0, 0, PACK)
        zero_window("first_stage")
        gather_words(2)
        first_product(0, 0, 0, r0, r2, True, False)
        first_product(4, 0, 0, r2, S, True, False)
        round_w1(0, 1, on_scalar, 0, SCALAR_SHARE_01)
        round_w1(0, 1, on_vector, SCALAR_SHARE_01, P)
        quantize_w1(0, 1, 0, PACK)
        first_product(0, 0, 1, r0, r2, False, False)
        round_w1(0, 2, on_scalar, 0, SCALAR_SHARE_02)
        round_in_pairs(0, 2, SCALAR_SHARE_02)
        first_product(0, 0, 2, r0, r2, False, True)
        first_product(4, 0, 2, r2, S, False, False)
        first_product(4, 0, 1, r2, S, False, True)

        round_w1(1, 0, on_scalar, 0, SCALAR_SHARE_10)
        round_w1(1, 0, on_vector, SCALAR_SHARE_10, P // 2)
        round_w1(1, 0, on_vector, P // 2, P)
        quantize_w1(1, 0, 0, PACK)
        round_in_pairs(1, 1, 0)
        round_w1(1, 2, on_scalar, 0, P // 2)
        round_in_pairs(1, 2, P // 2)
        drain_clip(planes0_front, 0, 0, range(PACK), front)

        all_passes(0, 1, r0, r1)
        last_t = PACK - 1
        nc.vector.tensor_scalar(first[last_t], bank[last_t][:, :NARROW], row_consts[:, last_t, 1, 0:1], None, ALU.add)
        for t in range(last_t):
            drain(0, 1, t, first[t])
        for t in range(PACK):
            drain(4, 0, t, back[t])
        weave(on_scalar, woven0_first.rearrange("p (c t) -> p c t", t=PACK), planes0_front, 0)
        for t in (0, last_t, 1, 2):
            clip(planes1_first, 1, t, first[t])
        weave(on_vector, lower[1], planes1_first, 0)
        quantize_h(stage_flat[1], 1, r0, r1)
        quantize_h(woven0_first, 0, r0, r1)
        for t in range(PACK):
            clip(planes0_back, 0, t, back[t])
        all_passes(4, 1, r1, r2)
        drain_clip(planes1_second, 4, 1, range(PACK), front_narrow)
        first_products = (first_weighted[:], y_sb[1][:, r0:r1])
        for nt, product in enumerate(first_products):
            second_product(nt, r0, r1)
            nc.vector.scalar_tensor_tensor(product, bank[nt][:, :NARROW], f0_sb[:, nt:nt + 1], wgo_sb[:, r0:r1],
                                           ALU.add, ALU.mult)
        for nt, product in enumerate(first_products):
            nc.vector.tensor_copy(places(nt, r0, r1), product)
        across_units = in_turn[:, 7 * NARROW // 2:9 * NARROW // 2]
        across_ranges = stage_flat[0].bitcast(F32)[:, 3 * NARROW // 2:5 * NARROW // 2]
        forces(2, r0, r1, across_units, across_ranges)

        def drain_clip_back(t, bank_number, engine):
            for a in range(KP):
                first_product(bank_number - t, 1, a, r2, S, a == 0, a == KP - 1, [t])
            drain(bank_number - t, 1, t, back[t])
            clip(planes1_back, 1, t, back[t], engine)

        weave(on_scalar, second_woven[:, 1, :, :], planes0_front, NARROW)
        weave(on_scalar, second_woven[:, 0, :, :], planes1_second, 0)
        nc.vector.quantize_mx(out=second_codes[:].bitcast(FP8X4), scales=second_sc[:], in_=second_flat)
        drain_clip_back(0, 4, nc.gpsimd)
        drain_clip_back(3, 5, nc.gpsimd)
        drain_clip_back(1, 6, nc.gpsimd)
        forces(3, r0, r1, y_on_planes(planes1_second))
        drain_clip_back(2, 2, nc.vector)

        forces(0, r1, r2, y_sb[0][:, r1:r2])
        weave(on_scalar, lower[0], planes0_back, 0)
        weave(on_scalar, upper[0], planes0_back, NARROW)
        quantize_h(stage_flat[0], 0, r2, S)
        forces(1, r1, r2, y_sb[1][:, r1:r2])
        weave(on_scalar, lower[2], planes1_back, 0)
        forces(2, r1, r2, y_sb[2][:, r1:r2])
        weave(on_scalar, upper[2], planes1_back, NARROW)
        quantize_h(stage_flat[2], 1, r2, S)
        forces(3, r1, r2, y_on_planes(planes1_back))

        forces(0, r2, r3, y_sb[0][:, r2:r3])
        for nt, j0 in ((1, r2), (0, r3), (2, r2), (3, r2)):
            forces(nt, j0, S, y_sb[nt][:, j0:])
            nc.sync.dma_start(out[nt * P:(nt + 1) * P, :], window[nt][:])
